import numpy as np
import ml_dtypes


def mxq(x, axis, fmt="e4m3"):
    dtype, down = {"e4m3": (ml_dtypes.float8_e4m3fn, 7), "e5m2": (ml_dtypes.float8_e5m2, 14)}[fmt]
    v = np.moveaxis(np.asarray(x, np.float32).astype(ml_dtypes.bfloat16).astype(np.float64), axis, -1)
    blocks = v.reshape(v.shape[:-1] + (-1, 32))
    amax = np.abs(blocks).max(-1, keepdims=True)
    byte = np.maximum(np.where(amax > 0, np.frexp(amax)[1] - 1 + 127, 0) - down, 1)
    scale = np.exp2(byte - 127.0)
    codes = (blocks / scale).astype(np.float32).astype(dtype).astype(np.float64)
    return np.moveaxis((codes * scale).reshape(v.shape), -1, axis)


WIDE = False


def mx_kscale(k, group=512):
    if not WIDE:
        return np.ones(k)
    levels = np.array([18, -18])
    if group != 512:
        return np.exp2(np.random.permutation(np.resize(levels, k // group))).repeat(group)
    if k % 512:
        return np.exp2(np.random.permutation(np.resize(levels, k // 32))).repeat(32)
    a = np.empty((k // 512, 16))
    for p in range(k // 512):
        a[p, :8] = np.random.permutation(np.resize(levels, 8))
        for g in range(8):
            far = levels[np.abs(levels - a[p, g]) >= 10]
            a[p, g + 8] = far[np.random.randint(len(far))]
    return np.exp2(a.ravel()).repeat(32)


def f64(x):
    return np.asarray(x).astype(np.float64)


G, D, M, N, L = 4, 128, 128, 512, 768


def setup_inputs():
    n = np.random.standard_normal
    s_d = mx_kscale(D, 0)
    return {
        "x": (n((G, D, L)) * s_d[:, None]).astype(np.float32),
        "w0": (n((G, D, M)) / np.sqrt(3 * D) / s_d[:, None]).astype(np.float32),
        "w1": (n((G, D, M)) / np.sqrt(3 * D) / s_d[:, None]).astype(np.float32),
        "w2": (n((G, D, M)) / np.sqrt(3 * D) / s_d[:, None]).astype(np.float32),
        "b": (0.5 * n((G, M, 1))).astype(np.float32),
    }


def reference(x, w0, w1, w2, b):
    w0q = mxq(f64(w0), 1, "e4m3")
    xq = mxq(f64(x), 1, "e4m3")
    w1q = mxq(f64(w1), 1, "e4m3")
    w2q = mxq(f64(w2), 1, "e4m3")
    z = (w0q.transpose(0, 2, 1) @ xq[..., :512]) + (w1q.transpose(0, 2, 1) @ xq[..., 128 : 640]) + (w2q.transpose(0, 2, 1) @ xq[..., 256 : 768])
    y = np.maximum(z + f64(b), 0.0)
    return y

@@ -1,0 +1,157 @@
+from contextlib import ExitStack
+
+import concourse.mybir as mybir
+
+G, D, M, N, L = 4, 128, 128, 512, 768
+TAPS = 3
+FLOPS = 2 * G * TAPS * D * M * N
+
+F32 = mybir.dt.float32
+BF16 = mybir.dt.bfloat16
+U32 = mybir.dt.uint32
+U8 = mybir.dt.uint8
+FP8X4 = mybir.dt.float8_e4m3fn_x4
+RELU = mybir.ActivationFunctionType.Relu
+ALU = mybir.AluOpType
+
+P = 128
+PACK = 4
+ROWS = D // PACK
+CH = 128
+BANK = 512
+X_LOADS = [(0, 2), (2, 1), (3, 1), (4, 1), (5, 1)]
+
+
+def tile_rows_conv_relu_kernel(tc, x, w0, w1, w2, b, out):
+    nc = tc.nc
+    x_rows = x.rearrange("g (p j) l -> (g p) j l", j=PACK)
+    w_rows = [w.rearrange("g (p j) m -> (g p) j m", j=PACK) for w in (w0, w1, w2)]
+    out_rows = out.rearrange("g m n -> m g n")
+
+    with ExitStack() as ctx:
+        sb = ctx.enter_context(tc.tile_pool(name="sb", bufs=1))
+        ps = ctx.enter_context(tc.psum_pool(name="ps", bufs=1))
+        ctx.enter_context(tc.manual_schedule())
+
+        x_raw = {c: sb.tile([P, PACK, n * CH], F32, name="x_raw%d" % c) for c, n in X_LOADS}
+        w_raw = [sb.tile([P, PACK, M], F32, name="w_raw%d" % t) for t in range(TAPS)]
+        x_bf = sb.tile([P, L, PACK], BF16, align_bytes=64, name="x_bf")
+        w_bf = sb.tile([P, TAPS, M, PACK], BF16, align_bytes=64, name="w_bf")
+        x_codes = sb.tile([P, L], U32, align_bytes=64, name="x_codes")
+        x_scales = sb.tile([P, L], U8, align_bytes=64, name="x_scales")
+        w_codes = sb.tile([P, TAPS, M], U32, align_bytes=64, name="w_codes")
+        w_scales = sb.tile([P, TAPS, M], U8, align_bytes=64, name="w_scales")
+        bias = sb.tile([P, G, 8], F32, name="bias")
+        warm = sb.tile([P, 8], F32, name="warm")
+        y = [sb.tile([P, G, CH], F32, name="y%d" % c) for c in range(N // CH)]
+        acc = [[ps.tile([P, BANK], F32, name="acc%d_%d" % (g, s)) for s in range(2)] for g in range(G)]
+
+        def load_x(i):
+            c, n = X_LOADS[i]
+            nc.sync.dma_start(out=x_raw[c][:], in_=x_rows[:, :, c * CH : (c + n) * CH])
+
+        def cast(eng, dst, src):
+            src = src.rearrange("p j (c i) -> p c j i", i=4)
+            dst = dst.rearrange("p (c i) j -> p c j i", i=4)
+            if eng == "v":
+                nc.vector.tensor_copy(out=dst, in_=src)
+            else:
+                nc.scalar.copy(out=dst, in_=src)
+
+        def cast_x(eng, i, part=0, parts=1):
+            c, n = X_LOADS[i]
+            w = n * CH // parts
+            cast(eng, x_bf[:, c * CH + part * w : c * CH + (part + 1) * w, :], x_raw[c][:, :, part * w : (part + 1) * w])
+
+        def quant_x(i, part=0, parts=1):
+            c, n = X_LOADS[i]
+            w = n * CH // parts
+            cols = slice(c * CH + part * w, c * CH + (part + 1) * w)
+            nc.vector.quantize_mx(out=x_codes[:, cols].bitcast(FP8X4), scales=x_scales[:, cols],
+                                  in_=x_bf[:, cols, :].rearrange("p w j -> p (w j)"))
+
+        def quant_w(t):
+            nc.vector.quantize_mx(out=w_codes[:, t, :].bitcast(FP8X4), scales=w_scales[:, t, :],
+                                  in_=w_bf[:, t, :, :].rearrange("p w j -> p (w j)"))
+
+        def sums(c, g):
+            return acc[g][c % 2][:, (c // 2) * CH : (c // 2 + 1) * CH]
+
+        def tap(c, t):
+            cols = slice((c + t) * CH, (c + t + 1) * CH)
+            for g in range(G):
+                rows = slice(g * ROWS, (g + 1) * ROWS)
+                nc.tensor.matmul_mx(
+                    out=sums(c, g),
+                    lhsT=w_codes[rows, t, :].bitcast(FP8X4),
+                    lhsT_scale=w_scales[rows, t, :],
+                    rhs=x_codes[rows, cols].bitcast(FP8X4),
+                    rhs_scale=x_scales[rows, cols],
+                    start=(t == 0),
+                    stop=(t == TAPS - 1),
+                )
+
+        def finish(eng, c, g):
+            if eng == "v":
+                nc.vector.tensor_scalar(out=y[c][:, g, :], in0=sums(c, g), scalar1=bias[:, g, 0:1],
+                                        scalar2=0.0, op0=ALU.add, op1=ALU.max)
+            else:
+                nc.scalar.activation(out=y[c][:, g, :], in_=sums(c, g), func=RELU, bias=bias[:, g, 0:1])
+
+        def store(c, g0=0, g1=G):
+            nc.sync.dma_start(out=out_rows[:, g0:g1, c * CH : (c + 1) * CH], in_=y[c][:, g0:g1, :])
+
+        def halves(i):
+            cast_x("v", i, 0, 2)
+            cast_x("v", i, 1, 2)
+            quant_x(i, 0, 2)
+            quant_x(i, 1, 2)
+
+        load_x(0)
+        with nc.allow_non_contiguous_dma(reason="one bias value for each partition and group"):
+            nc.scalar.dma_start(out=bias[:, :, 0:1], in_=b.rearrange("g m o -> m g o"))
+        for t in range(TAPS):
+            nc.sync.dma_start(out=w_raw[t][:], in_=w_rows[t])
+        for i in range(1, len(X_LOADS)):
+            load_x(i)
+
+        nc.vector.memset(warm[:], 0.0)
+        nc.scalar.activation(out=warm[:, 1:2], in_=warm[:, 0:1], func=RELU)
+
+        cast("s", w_bf[:, 0, :, :], w_raw[0][:])
+        halves(0)
+        cast("v", w_bf[:, 1, :, :], w_raw[1][:])
+        quant_w(0)
+        cast("s", w_bf[:, 2, :, :], w_raw[2][:])
+        quant_w(1)
+        tap(0, 0)
+        tap(1, 0)
+        tap(0, 1)
+        cast_x("v", 1)
+        quant_w(2)
+        quant_x(1)
+        tap(0, 2)
+        tap(1, 1)
+        for g in range(G):
+            finish("s", 0, g)
+        store(0)
+        halves(2)
+        tap(1, 2)
+        tap(2, 0)
+        tap(2, 1)
+        for g in range(G):
+            finish("s", 1, g)
+        store(1)
+        halves(3)
+        tap(2, 2)
+        tap(3, 0)
+        tap(3, 1)
+        for g in range(G):
+            finish("s", 2, g)
+        store(2)
+        halves(4)
+        tap(3, 2)
+        for g in range(G):
+            finish("sv"[g % 2], 3, g)
+            if g % 2 == 1:
+                store(3, g - 1, g + 1)

@@ -19,7 +19,7 @@ PACK = 4
 ROWS = D // PACK
 CH = 128
 BANK = 512
-X_LOADS = [(0, 2), (2, 1), (3, 1), (4, 1), (5, 1)]
+X_LOADS = [(c, 1) for c in range(6)]
 
 
 def tile_rows_conv_relu_kernel(tc, x, w0, w1, w2, b, out):
@@ -107,50 +107,49 @@ def tile_rows_conv_relu_kernel(tc, x, w0, w1, w2, b, out):
             quant_x(i, 0, 2)
             quant_x(i, 1, 2)
 
-        load_x(0)
-        with nc.allow_non_contiguous_dma(reason="one bias value for each partition and group"):
-            nc.scalar.dma_start(out=bias[:, :, 0:1], in_=b.rearrange("g m o -> m g o"))
-        for t in range(TAPS):
+        def load_w(t):
             nc.sync.dma_start(out=w_raw[t][:], in_=w_rows[t])
-        for i in range(1, len(X_LOADS)):
-            load_x(i)
+
+        load_w(0)
+        load_x(0)
+        load_x(1)
+        load_w(1)
+        load_x(2)
+        load_w(2)
+        load_x(3)
+        load_x(4)
+        load_x(5)
 
         nc.vector.memset(warm[:], 0.0)
         nc.scalar.activation(out=warm[:, 1:2], in_=warm[:, 0:1], func=RELU)
+        with nc.allow_non_contiguous_dma(reason="one bias value for each partition and group"):
+            nc.scalar.dma_start(out=bias[:, :, 0:1], in_=b.rearrange("g m o -> m g o"))
 
-        cast("s", w_bf[:, 0, :, :], w_raw[0][:])
-        halves(0)
-        cast("v", w_bf[:, 1, :, :], w_raw[1][:])
+        cast("v", w_bf[:, 0, :, :], w_raw[0][:])
         quant_w(0)
-        cast("s", w_bf[:, 2, :, :], w_raw[2][:])
-        quant_w(1)
+        cast_x("v", 0, 0, 2)
+        cast_x("s", 0, 1, 2)
+        quant_x(0)
         tap(0, 0)
+        halves(1)
         tap(1, 0)
+        cast("s", w_bf[:, 1, :, :], w_raw[1][:])
+        quant_w(1)
         tap(0, 1)
-        cast_x("v", 1)
-        quant_w(2)
-        quant_x(1)
-        tap(0, 2)
-        tap(1, 1)
-        for g in range(G):
-            finish("s", 0, g)
-        store(0)
         halves(2)
-        tap(1, 2)
-        tap(2, 0)
-        tap(2, 1)
-        for g in range(G):
-            finish("s", 1, g)
-        store(1)
-        halves(3)
-        tap(2, 2)
-        tap(3, 0)
-        tap(3, 1)
-        for g in range(G):
-            finish("s", 2, g)
-        store(2)
-        halves(4)
-        tap(3, 2)
+        tap(1, 1)
+        cast("s", w_bf[:, 2, :, :], w_raw[2][:])
+        quant_w(2)
+        tap(0, 2)
+        for c in range(3):
+            for g in range(G):
+                finish("s", c, g)
+            store(c)
+            halves(c + 3)
+            tap(c + 1, 2)
+            if c < 2:
+                tap(c + 2, 0)
+                tap(c + 2, 1)
         for g in range(G):
             finish("sv"[g % 2], 3, g)
             if g % 2 == 1:

@@ -41,7 +41,8 @@ def tile_rows_conv_relu_kernel(tc, x, w0, w1, w2, b, out):
         x_scales = sb.tile([P, L], U8, align_bytes=64, name="x_scales")
         w_codes = sb.tile([P, TAPS, M], U32, align_bytes=64, name="w_codes")
         w_scales = sb.tile([P, TAPS, M], U8, align_bytes=64, name="w_scales")
-        bias = sb.tile([P, G, 8], F32, name="bias")
+        bias_rows = sb.tile([P, G * ROWS], F32, align_bytes=64, name="bias_rows")
+        bias = sb.tile([P, G * ROWS], F32, align_bytes=64, name="bias")
         warm = sb.tile([P, 8], F32, name="warm")
         y = [sb.tile([P, G, CH], F32, name="y%d" % c) for c in range(N // CH)]
         acc = [[ps.tile([P, BANK], F32, name="acc%d_%d" % (g, s)) for s in range(2)] for g in range(G)]
@@ -93,10 +94,10 @@ def tile_rows_conv_relu_kernel(tc, x, w0, w1, w2, b, out):
 
         def finish(eng, c, g):
             if eng == "v":
-                nc.vector.tensor_scalar(out=y[c][:, g, :], in0=sums(c, g), scalar1=bias[:, g, 0:1],
+                nc.vector.tensor_scalar(out=y[c][:, g, :], in0=sums(c, g), scalar1=bias[:, g * ROWS : g * ROWS + 1],
                                         scalar2=0.0, op0=ALU.add, op1=ALU.max)
             else:
-                nc.scalar.activation(out=y[c][:, g, :], in_=sums(c, g), func=RELU, bias=bias[:, g, 0:1])
+                nc.scalar.activation(out=y[c][:, g, :], in_=sums(c, g), func=RELU, bias=bias[:, g * ROWS : g * ROWS + 1])
 
         def store(c, g0=0, g1=G):
             nc.sync.dma_start(out=out_rows[:, g0:g1, c * CH : (c + 1) * CH], in_=y[c][:, g0:g1, :])
@@ -110,6 +111,9 @@ def tile_rows_conv_relu_kernel(tc, x, w0, w1, w2, b, out):
         def load_w(t):
             nc.sync.dma_start(out=w_raw[t][:], in_=w_rows[t])
 
+        nc.vector.memset(bias_rows[:], 0.0)
+        nc.scalar.dma_start(out=bias_rows[0:P:ROWS, :].rearrange("q (g j) -> q g j", g=G),
+                            in_=b.rearrange("g (q j) o -> q g (j o)", j=ROWS))
         load_w(0)
         load_x(0)
         load_x(1)
@@ -122,8 +126,6 @@ def tile_rows_conv_relu_kernel(tc, x, w0, w1, w2, b, out):
 
         nc.vector.memset(warm[:], 0.0)
         nc.scalar.activation(out=warm[:, 1:2], in_=warm[:, 0:1], func=RELU)
-        with nc.allow_non_contiguous_dma(reason="one bias value for each partition and group"):
-            nc.scalar.dma_start(out=bias[:, :, 0:1], in_=b.rearrange("g m o -> m g o"))
 
         cast("v", w_bf[:, 0, :, :], w_raw[0][:])
         quant_w(0)
@@ -134,6 +136,7 @@ def tile_rows_conv_relu_kernel(tc, x, w0, w1, w2, b, out):
         halves(1)
         tap(1, 0)
         cast("s", w_bf[:, 1, :, :], w_raw[1][:])
+        nc.vector.transpose(out=bias[:], in_=bias_rows[:])
         quant_w(1)
         tap(0, 1)
         halves(2)

@@ -11,29 +11,35 @@ BF16 = mybir.dt.bfloat16
 U32 = mybir.dt.uint32
 U8 = mybir.dt.uint8
 FP8X4 = mybir.dt.float8_e4m3fn_x4
+COPY = mybir.ActivationFunctionType.Copy
 RELU = mybir.ActivationFunctionType.Relu
 ALU = mybir.AluOpType
 
 P = 128
 PACK = 4
 ROWS = D // PACK
-CH = 128
+CHUNK = 128
+X_CHUNKS = L // CHUNK
+OUT_CHUNKS = N // CHUNK
 BANK = 512
-X_LOADS = [(c, 1) for c in range(6)]
+OPEN = 2
+RUN = 4
+PAIR = 2
 
 
 def tile_rows_conv_relu_kernel(tc, x, w0, w1, w2, b, out):
     nc = tc.nc
     x_rows = x.rearrange("g (p j) l -> (g p) j l", j=PACK)
-    w_rows = [w.rearrange("g (p j) m -> (g p) j m", j=PACK) for w in (w0, w1, w2)]
     out_rows = out.rearrange("g m n -> m g n")
+    w_rows = [w.rearrange("g (p j) m -> (g p) j m", j=PACK) for w in (w0, w1, w2)]
 
     with ExitStack() as ctx:
         sb = ctx.enter_context(tc.tile_pool(name="sb", bufs=1))
         ps = ctx.enter_context(tc.psum_pool(name="ps", bufs=1))
         ctx.enter_context(tc.manual_schedule())
 
-        x_raw = {c: sb.tile([P, PACK, n * CH], F32, name="x_raw%d" % c) for c, n in X_LOADS}
+        x_first = sb.tile([P, PACK, TAPS * CHUNK], F32, name="x_first")
+        x_late = {c: sb.tile([P, PACK, CHUNK], F32, name="x_late%d" % c) for c in range(TAPS, X_CHUNKS)}
         w_raw = [sb.tile([P, PACK, M], F32, name="w_raw%d" % t) for t in range(TAPS)]
         x_bf = sb.tile([P, L, PACK], BF16, align_bytes=64, name="x_bf")
         w_bf = sb.tile([P, TAPS, M, PACK], BF16, align_bytes=64, name="w_bf")
@@ -43,43 +49,46 @@ def tile_rows_conv_relu_kernel(tc, x, w0, w1, w2, b, out):
         w_scales = sb.tile([P, TAPS, M], U8, align_bytes=64, name="w_scales")
         bias_rows = sb.tile([P, G * ROWS], F32, align_bytes=64, name="bias_rows")
         bias = sb.tile([P, G * ROWS], F32, align_bytes=64, name="bias")
-        warm = sb.tile([P, 8], F32, name="warm")
-        y = [sb.tile([P, G, CH], F32, name="y%d" % c) for c in range(N // CH)]
-        acc = [[ps.tile([P, BANK], F32, name="acc%d_%d" % (g, s)) for s in range(2)] for g in range(G)]
+        y = [sb.tile([P, G, CHUNK], F32, name="y%d" % c) for c in range(OUT_CHUNKS)]
+        acc = [[ps.tile([P, BANK], F32, name="acc%d_%d" % (g, s)) for s in range(OPEN)] for g in range(G)]
 
-        def load_x(i):
-            c, n = X_LOADS[i]
-            nc.sync.dma_start(out=x_raw[c][:], in_=x_rows[:, :, c * CH : (c + n) * CH])
-
-        def cast(eng, dst, src):
-            src = src.rearrange("p j (c i) -> p c j i", i=4)
-            dst = dst.rearrange("p (c i) j -> p c j i", i=4)
-            if eng == "v":
+        def interleave(on_vector, dst, src):
+            src = src.rearrange("p j (c i) -> p c j i", i=RUN)
+            dst = dst.rearrange("p (c i) j -> p c j i", i=RUN)
+            if on_vector:
                 nc.vector.tensor_copy(out=dst, in_=src)
             else:
-                nc.scalar.copy(out=dst, in_=src)
+                nc.scalar.activation(out=dst, in_=src, func=COPY)
 
-        def cast_x(eng, i, part=0, parts=1):
-            c, n = X_LOADS[i]
-            w = n * CH // parts
-            cast(eng, x_bf[:, c * CH + part * w : c * CH + (part + 1) * w, :], x_raw[c][:, :, part * w : (part + 1) * w])
+        def interleave_w(on_vector, t, m0, m1):
+            interleave(on_vector, w_bf[:, t, m0:m1, :], w_raw[t][:, :, m0:m1])
 
-        def quant_x(i, part=0, parts=1):
-            c, n = X_LOADS[i]
-            w = n * CH // parts
-            cols = slice(c * CH + part * w, c * CH + (part + 1) * w)
-            nc.vector.quantize_mx(out=x_codes[:, cols].bitcast(FP8X4), scales=x_scales[:, cols],
-                                  in_=x_bf[:, cols, :].rearrange("p w j -> p (w j)"))
+        def quantize_x(lo, hi):
+            nc.vector.quantize_mx(
+                out=x_codes[:, lo:hi].bitcast(FP8X4),
+                scales=x_scales[:, lo:hi],
+                in_=x_bf[:, lo:hi, :].rearrange("p w j -> p (w j)"),
+            )
 
-        def quant_w(t):
-            nc.vector.quantize_mx(out=w_codes[:, t, :].bitcast(FP8X4), scales=w_scales[:, t, :],
-                                  in_=w_bf[:, t, :, :].rearrange("p w j -> p (w j)"))
+        def quantize_w(t):
+            nc.vector.quantize_mx(
+                out=w_codes[:, t, :].bitcast(FP8X4),
+                scales=w_scales[:, t, :],
+                in_=w_bf[:, t, :, :].rearrange("p w j -> p (w j)"),
+            )
+
+        def prepare_late_x(c):
+            half = CHUNK // 2
+            for h in (0, half):
+                interleave(True, x_bf[:, c * CHUNK + h : c * CHUNK + h + half, :], x_late[c][:, :, h : h + half])
+            for h in (0, half):
+                quantize_x(c * CHUNK + h, c * CHUNK + h + half)
 
         def sums(c, g):
-            return acc[g][c % 2][:, (c // 2) * CH : (c // 2 + 1) * CH]
+            return acc[g][c % OPEN][:, (c // OPEN) * CHUNK : (c // OPEN + 1) * CHUNK]
 
         def tap(c, t):
-            cols = slice((c + t) * CH, (c + t + 1) * CH)
+            cols = slice((c + t) * CHUNK, (c + t + 1) * CHUNK)
             for g in range(G):
                 rows = slice(g * ROWS, (g + 1) * ROWS)
                 nc.tensor.matmul_mx(
@@ -92,68 +101,52 @@ def tile_rows_conv_relu_kernel(tc, x, w0, w1, w2, b, out):
                     stop=(t == TAPS - 1),
                 )
 
-        def finish(eng, c, g):
-            if eng == "v":
-                nc.vector.tensor_scalar(out=y[c][:, g, :], in0=sums(c, g), scalar1=bias[:, g * ROWS : g * ROWS + 1],
-                                        scalar2=0.0, op0=ALU.add, op1=ALU.max)
-            else:
-                nc.scalar.activation(out=y[c][:, g, :], in_=sums(c, g), func=RELU, bias=bias[:, g * ROWS : g * ROWS + 1])
-
-        def store(c, g0=0, g1=G):
-            nc.sync.dma_start(out=out_rows[:, g0:g1, c * CH : (c + 1) * CH], in_=y[c][:, g0:g1, :])
-
-        def halves(i):
-            cast_x("v", i, 0, 2)
-            cast_x("v", i, 1, 2)
-            quant_x(i, 0, 2)
-            quant_x(i, 1, 2)
-
-        def load_w(t):
-            nc.sync.dma_start(out=w_raw[t][:], in_=w_rows[t])
-
-        nc.vector.memset(bias_rows[:], 0.0)
-        nc.scalar.dma_start(out=bias_rows[0:P:ROWS, :].rearrange("q (g j) -> q g j", g=G),
-                            in_=b.rearrange("g (q j) o -> q g (j o)", j=ROWS))
-        load_w(0)
-        load_x(0)
-        load_x(1)
-        load_w(1)
-        load_x(2)
-        load_w(2)
-        load_x(3)
-        load_x(4)
-        load_x(5)
-
-        nc.vector.memset(warm[:], 0.0)
-        nc.scalar.activation(out=warm[:, 1:2], in_=warm[:, 0:1], func=RELU)
-
-        cast("v", w_bf[:, 0, :, :], w_raw[0][:])
-        quant_w(0)
-        cast_x("v", 0, 0, 2)
-        cast_x("s", 0, 1, 2)
-        quant_x(0)
-        tap(0, 0)
-        halves(1)
-        tap(1, 0)
-        cast("s", w_bf[:, 1, :, :], w_raw[1][:])
-        nc.vector.transpose(out=bias[:], in_=bias_rows[:])
-        quant_w(1)
-        tap(0, 1)
-        halves(2)
-        tap(1, 1)
-        cast("s", w_bf[:, 2, :, :], w_raw[2][:])
-        quant_w(2)
-        tap(0, 2)
-        for c in range(3):
+        def finish(c, share_with_vector):
             for g in range(G):
-                finish("s", c, g)
-            store(c)
-            halves(c + 3)
-            tap(c + 1, 2)
-            if c < 2:
-                tap(c + 2, 0)
-                tap(c + 2, 1)
-        for g in range(G):
-            finish("sv"[g % 2], 3, g)
-            if g % 2 == 1:
-                store(3, g - 1, g + 1)
+                bias_g = bias[:, g * ROWS : g * ROWS + 1]
+                if share_with_vector and g % PAIR == 1:
+                    nc.vector.tensor_scalar(
+                        out=y[c][:, g, :], in0=sums(c, g), scalar1=bias_g, scalar2=0.0, op0=ALU.add, op1=ALU.max
+                    )
+                else:
+                    nc.scalar.activation(out=y[c][:, g, :], in_=sums(c, g), func=RELU, bias=bias_g)
+                if g % PAIR == PAIR - 1:
+                    groups = slice(g + 1 - PAIR, g + 1)
+                    nc.sync.dma_start(out=out_rows[:, groups, c * CHUNK : (c + 1) * CHUNK], in_=y[c][:, groups, :])
+
+        nc.sync.dma_start(out=x_first[:], in_=x_rows[:, :, : TAPS * CHUNK])
+        nc.vector.memset(bias_rows[:], 0.0)
+        nc.scalar.dma_start(
+            out=bias_rows[0:P:ROWS, :].rearrange("q (g j) -> q g j", g=G),
+            in_=b.rearrange("g (q j) o -> q g (j o)", j=ROWS),
+        )
+        for t in range(TAPS):
+            nc.sync.dma_start(out=w_raw[t][:], in_=w_rows[t])
+        for c in range(TAPS, X_CHUNKS):
+            nc.sync.dma_start(out=x_late[c][:], in_=x_rows[:, :, c * CHUNK : (c + 1) * CHUNK])
+
+        interleave(True, x_bf[:, : 2 * CHUNK, :], x_first[:, :, : 2 * CHUNK])
+        interleave(False, x_bf[:, 2 * CHUNK : 3 * CHUNK, :], x_first[:, :, 2 * CHUNK :])
+        quantize_x(0, 2 * CHUNK)
+        interleave_w(False, 0, 0, M)
+        quantize_x(2 * CHUNK, 3 * CHUNK)
+        quantize_w(0)
+        tap(0, 0)
+        tap(1, 0)
+        for t in range(1, TAPS):
+            interleave_w(True, t, 0, M // 2)
+            interleave_w(False, t, M // 2, M)
+            quantize_w(t)
+            tap(0, t)
+            if t < TAPS - 1:
+                tap(1, t)
+        nc.vector.transpose(out=bias[:], in_=bias_rows[:])
+
+        for c in range(OUT_CHUNKS - 1):
+            prepare_late_x(c + TAPS)
+            finish(c, share_with_vector=False)
+            tap(c + 1, TAPS - 1)
+            if c + OPEN < OUT_CHUNKS:
+                for t in range(TAPS - 1):
+                    tap(c + OPEN, t)
+        finish(OUT_CHUNKS - 1, share_with_vector=True)

@@ -24,7 +24,8 @@ OUT_CHUNKS = N // CHUNK
 BANK = 512
 OPEN = 2
 RUN = 4
-PAIR = 2
+W1_ON_VECTOR = 32
+W2_ON_VECTOR = 80
 
 
 def tile_rows_conv_relu_kernel(tc, x, w0, w1, w2, b, out):
@@ -104,15 +105,13 @@ def tile_rows_conv_relu_kernel(tc, x, w0, w1, w2, b, out):
         def finish(c, share_with_vector):
             for g in range(G):
                 bias_g = bias[:, g * ROWS : g * ROWS + 1]
-                if share_with_vector and g % PAIR == 1:
+                if share_with_vector and g % 2 == 1:
                     nc.vector.tensor_scalar(
                         out=y[c][:, g, :], in0=sums(c, g), scalar1=bias_g, scalar2=0.0, op0=ALU.add, op1=ALU.max
                     )
                 else:
                     nc.scalar.activation(out=y[c][:, g, :], in_=sums(c, g), func=RELU, bias=bias_g)
-                if g % PAIR == PAIR - 1:
-                    groups = slice(g + 1 - PAIR, g + 1)
-                    nc.sync.dma_start(out=out_rows[:, groups, c * CHUNK : (c + 1) * CHUNK], in_=y[c][:, groups, :])
+                nc.sync.dma_start(out=out_rows[:, g, c * CHUNK : (c + 1) * CHUNK], in_=y[c][:, g, :])
 
         nc.sync.dma_start(out=x_first[:], in_=x_rows[:, :, : TAPS * CHUNK])
         nc.vector.memset(bias_rows[:], 0.0)
@@ -125,22 +124,25 @@ def tile_rows_conv_relu_kernel(tc, x, w0, w1, w2, b, out):
         for c in range(TAPS, X_CHUNKS):
             nc.sync.dma_start(out=x_late[c][:], in_=x_rows[:, :, c * CHUNK : (c + 1) * CHUNK])
 
-        interleave(True, x_bf[:, : 2 * CHUNK, :], x_first[:, :, : 2 * CHUNK])
+        interleave(True, x_bf[:, :CHUNK, :], x_first[:, :, :CHUNK])
+        interleave(True, x_bf[:, CHUNK : 2 * CHUNK, :], x_first[:, :, CHUNK : 2 * CHUNK])
         interleave(False, x_bf[:, 2 * CHUNK : 3 * CHUNK, :], x_first[:, :, 2 * CHUNK :])
-        quantize_x(0, 2 * CHUNK)
         interleave_w(False, 0, 0, M)
-        quantize_x(2 * CHUNK, 3 * CHUNK)
+        for c in range(TAPS):
+            quantize_x(c * CHUNK, (c + 1) * CHUNK)
         quantize_w(0)
         tap(0, 0)
         tap(1, 0)
-        for t in range(1, TAPS):
-            interleave_w(True, t, 0, M // 2)
-            interleave_w(False, t, M // 2, M)
-            quantize_w(t)
-            tap(0, t)
-            if t < TAPS - 1:
-                tap(1, t)
+        interleave_w(True, 1, 0, W1_ON_VECTOR)
+        interleave_w(False, 1, W1_ON_VECTOR, M)
         nc.vector.transpose(out=bias[:], in_=bias_rows[:])
+        interleave_w(True, 2, 0, W2_ON_VECTOR)
+        interleave_w(False, 2, W2_ON_VECTOR, M)
+        quantize_w(1)
+        quantize_w(2)
+        tap(0, 1)
+        tap(0, 2)
+        tap(1, 1)
 
         for c in range(OUT_CHUNKS - 1):
             prepare_late_x(c + TAPS)

@@ -24,7 +24,6 @@ OUT_CHUNKS = N // CHUNK
 BANK = 512
 OPEN = 2
 RUN = 4
-W1_ON_VECTOR = 32
 W2_ON_VECTOR = 80
 
 
@@ -88,9 +87,9 @@ def tile_rows_conv_relu_kernel(tc, x, w0, w1, w2, b, out):
         def sums(c, g):
             return acc[g][c % OPEN][:, (c // OPEN) * CHUNK : (c // OPEN + 1) * CHUNK]
 
-        def tap(c, t):
+        def tap(c, t, groups=range(G)):
             cols = slice((c + t) * CHUNK, (c + t + 1) * CHUNK)
-            for g in range(G):
+            for g in groups:
                 rows = slice(g * ROWS, (g + 1) * ROWS)
                 nc.tensor.matmul_mx(
                     out=sums(c, g),
@@ -102,10 +101,10 @@ def tile_rows_conv_relu_kernel(tc, x, w0, w1, w2, b, out):
                     stop=(t == TAPS - 1),
                 )
 
-        def finish(c, share_with_vector):
+        def finish(c, on_vector):
             for g in range(G):
                 bias_g = bias[:, g * ROWS : g * ROWS + 1]
-                if share_with_vector and g % 2 == 1:
+                if g in on_vector:
                     nc.vector.tensor_scalar(
                         out=y[c][:, g, :], in0=sums(c, g), scalar1=bias_g, scalar2=0.0, op0=ALU.add, op1=ALU.max
                     )
@@ -113,29 +112,29 @@ def tile_rows_conv_relu_kernel(tc, x, w0, w1, w2, b, out):
                     nc.scalar.activation(out=y[c][:, g, :], in_=sums(c, g), func=RELU, bias=bias_g)
                 nc.sync.dma_start(out=out_rows[:, g, c * CHUNK : (c + 1) * CHUNK], in_=y[c][:, g, :])
 
-        nc.sync.dma_start(out=x_first[:], in_=x_rows[:, :, : TAPS * CHUNK])
+        nc.sync.dma_start(out=w_raw[0][:], in_=w_rows[0])
         nc.vector.memset(bias_rows[:], 0.0)
-        nc.scalar.dma_start(
+        nc.sync.dma_start(
             out=bias_rows[0:P:ROWS, :].rearrange("q (g j) -> q g j", g=G),
             in_=b.rearrange("g (q j) o -> q g (j o)", j=ROWS),
         )
-        for t in range(TAPS):
+        nc.sync.dma_start(out=x_first[:], in_=x_rows[:, :, : TAPS * CHUNK])
+        for t in range(1, TAPS):
             nc.sync.dma_start(out=w_raw[t][:], in_=w_rows[t])
         for c in range(TAPS, X_CHUNKS):
             nc.sync.dma_start(out=x_late[c][:], in_=x_rows[:, :, c * CHUNK : (c + 1) * CHUNK])
 
+        interleave_w(True, 0, 0, M)
+        nc.vector.transpose(out=bias[:], in_=bias_rows[:])
+        quantize_w(0)
         interleave(True, x_bf[:, :CHUNK, :], x_first[:, :, :CHUNK])
         interleave(True, x_bf[:, CHUNK : 2 * CHUNK, :], x_first[:, :, CHUNK : 2 * CHUNK])
         interleave(False, x_bf[:, 2 * CHUNK : 3 * CHUNK, :], x_first[:, :, 2 * CHUNK :])
-        interleave_w(False, 0, 0, M)
         for c in range(TAPS):
             quantize_x(c * CHUNK, (c + 1) * CHUNK)
-        quantize_w(0)
         tap(0, 0)
         tap(1, 0)
-        interleave_w(True, 1, 0, W1_ON_VECTOR)
-        interleave_w(False, 1, W1_ON_VECTOR, M)
-        nc.vector.transpose(out=bias[:], in_=bias_rows[:])
+        interleave_w(False, 1, 0, M)
         interleave_w(True, 2, 0, W2_ON_VECTOR)
         interleave_w(False, 2, W2_ON_VECTOR, M)
         quantize_w(1)
@@ -146,9 +145,10 @@ def tile_rows_conv_relu_kernel(tc, x, w0, w1, w2, b, out):
 
         for c in range(OUT_CHUNKS - 1):
             prepare_late_x(c + TAPS)
-            finish(c, share_with_vector=False)
+            finish(c, on_vector=(2,))
             tap(c + 1, TAPS - 1)
             if c + OPEN < OUT_CHUNKS:
-                for t in range(TAPS - 1):
-                    tap(c + OPEN, t)
-        finish(OUT_CHUNKS - 1, share_with_vector=True)
+                for g in range(G):
+                    for t in range(TAPS - 1):
+                        tap(c + OPEN, t, [g])
+        finish(OUT_CHUNKS - 1, on_vector=(1, 3))

@@ -24,7 +24,6 @@ OUT_CHUNKS = N // CHUNK
 BANK = 512
 OPEN = 2
 RUN = 4
-W2_ON_VECTOR = 80
 
 
 def tile_rows_conv_relu_kernel(tc, x, w0, w1, w2, b, out):
@@ -38,9 +37,9 @@ def tile_rows_conv_relu_kernel(tc, x, w0, w1, w2, b, out):
         ps = ctx.enter_context(tc.psum_pool(name="ps", bufs=1))
         ctx.enter_context(tc.manual_schedule())
 
-        x_first = sb.tile([P, PACK, TAPS * CHUNK], F32, name="x_first")
-        x_late = {c: sb.tile([P, PACK, CHUNK], F32, name="x_late%d" % c) for c in range(TAPS, X_CHUNKS)}
-        w_raw = [sb.tile([P, PACK, M], F32, name="w_raw%d" % t) for t in range(TAPS)]
+        x_first = sb.tile([P, PACK, TAPS * CHUNK], F32, align_bytes=512, name="x_first")
+        x_late = {c: sb.tile([P, PACK, CHUNK], F32, align_bytes=512, name="x_late%d" % c) for c in range(TAPS, X_CHUNKS)}
+        w_raw = [sb.tile([P, PACK, M], F32, align_bytes=512, name="w_raw%d" % t) for t in range(TAPS)]
         x_bf = sb.tile([P, L, PACK], BF16, align_bytes=64, name="x_bf")
         w_bf = sb.tile([P, TAPS, M, PACK], BF16, align_bytes=64, name="w_bf")
         x_codes = sb.tile([P, L], U32, align_bytes=64, name="x_codes")
@@ -49,7 +48,7 @@ def tile_rows_conv_relu_kernel(tc, x, w0, w1, w2, b, out):
         w_scales = sb.tile([P, TAPS, M], U8, align_bytes=64, name="w_scales")
         bias_rows = sb.tile([P, G * ROWS], F32, align_bytes=64, name="bias_rows")
         bias = sb.tile([P, G * ROWS], F32, align_bytes=64, name="bias")
-        y = [sb.tile([P, G, CHUNK], F32, name="y%d" % c) for c in range(OUT_CHUNKS)]
+        y = [sb.tile([P, G, CHUNK], F32, align_bytes=512, name="y%d" % c) for c in range(OUT_CHUNKS)]
         acc = [[ps.tile([P, BANK], F32, name="acc%d_%d" % (g, s)) for s in range(OPEN)] for g in range(G)]
 
         def interleave(on_vector, dst, src):
@@ -70,11 +69,11 @@ def tile_rows_conv_relu_kernel(tc, x, w0, w1, w2, b, out):
                 in_=x_bf[:, lo:hi, :].rearrange("p w j -> p (w j)"),
             )
 
-        def quantize_w(t):
+        def quantize_w(t, m0, m1):
             nc.vector.quantize_mx(
-                out=w_codes[:, t, :].bitcast(FP8X4),
-                scales=w_scales[:, t, :],
-                in_=w_bf[:, t, :, :].rearrange("p w j -> p (w j)"),
+                out=w_codes[:, t, m0:m1].bitcast(FP8X4),
+                scales=w_scales[:, t, m0:m1],
+                in_=w_bf[:, t, m0:m1, :].rearrange("p w j -> p (w j)"),
             )
 
         def prepare_late_x(c):
@@ -126,7 +125,7 @@ def tile_rows_conv_relu_kernel(tc, x, w0, w1, w2, b, out):
 
         interleave_w(True, 0, 0, M)
         nc.vector.transpose(out=bias[:], in_=bias_rows[:])
-        quantize_w(0)
+        quantize_w(0, 0, M)
         interleave(True, x_bf[:, :CHUNK, :], x_first[:, :, :CHUNK])
         interleave(True, x_bf[:, CHUNK : 2 * CHUNK, :], x_first[:, :, CHUNK : 2 * CHUNK])
         interleave(False, x_bf[:, 2 * CHUNK : 3 * CHUNK, :], x_first[:, :, 2 * CHUNK :])
@@ -135,10 +134,11 @@ def tile_rows_conv_relu_kernel(tc, x, w0, w1, w2, b, out):
         tap(0, 0)
         tap(1, 0)
         interleave_w(False, 1, 0, M)
-        interleave_w(True, 2, 0, W2_ON_VECTOR)
-        interleave_w(False, 2, W2_ON_VECTOR, M)
-        quantize_w(1)
-        quantize_w(2)
+        interleave_w(True, 2, 0, M // 2)
+        interleave_w(True, 2, M // 2, M)
+        quantize_w(1, 0, M)
+        quantize_w(2, 0, M // 2)
+        quantize_w(2, M // 2, M)
         tap(0, 1)
         tap(0, 2)
         tap(1, 1)

@@ -100,7 +100,7 @@ def tile_rows_conv_relu_kernel(tc, x, w0, w1, w2, b, out):
                     stop=(t == TAPS - 1),
                 )
 
-        def finish(c, on_vector):
+        def finish(c, on_vector, stores):
             for g in range(G):
                 bias_g = bias[:, g * ROWS : g * ROWS + 1]
                 if g in on_vector:
@@ -109,7 +109,9 @@ def tile_rows_conv_relu_kernel(tc, x, w0, w1, w2, b, out):
                     )
                 else:
                     nc.scalar.activation(out=y[c][:, g, :], in_=sums(c, g), func=RELU, bias=bias_g)
-                nc.sync.dma_start(out=out_rows[:, g, c * CHUNK : (c + 1) * CHUNK], in_=y[c][:, g, :])
+                for groups in stores:
+                    if groups.stop == g + 1:
+                        nc.sync.dma_start(out=out_rows[:, groups, c * CHUNK : (c + 1) * CHUNK], in_=y[c][:, groups, :])
 
         nc.sync.dma_start(out=w_raw[0][:], in_=w_rows[0])
         nc.vector.memset(bias_rows[:], 0.0)
@@ -145,10 +147,10 @@ def tile_rows_conv_relu_kernel(tc, x, w0, w1, w2, b, out):
 
         for c in range(OUT_CHUNKS - 1):
             prepare_late_x(c + TAPS)
-            finish(c, on_vector=(2,))
+            finish(c, on_vector=(2,), stores=(slice(0, 1), slice(1, 2), slice(2, 4)))
             tap(c + 1, TAPS - 1)
             if c + OPEN < OUT_CHUNKS:
                 for g in range(G):
                     for t in range(TAPS - 1):
                         tap(c + OPEN, t, [g])
-        finish(OUT_CHUNKS - 1, on_vector=(1, 3))
+        finish(OUT_CHUNKS - 1, on_vector=(1, 3), stores=(slice(0, 2), slice(2, 4)))

@@ -147,7 +147,7 @@ def tile_rows_conv_relu_kernel(tc, x, w0, w1, w2, b, out):
 
         for c in range(OUT_CHUNKS - 1):
             prepare_late_x(c + TAPS)
-            finish(c, on_vector=(2,), stores=(slice(0, 1), slice(1, 2), slice(2, 4)))
+            finish(c, on_vector=(1,), stores=(slice(0, 1), slice(1, 4)))
             tap(c + 1, TAPS - 1)
             if c + OPEN < OUT_CHUNKS:
                 for g in range(G):

@@ -22,6 +22,7 @@ CHUNK = 128
 X_CHUNKS = L // CHUNK
 OUT_CHUNKS = N // CHUNK
 BANK = 512
+EARLY = 4
 OPEN = 2
 RUN = 4
 
@@ -37,8 +38,8 @@ def tile_rows_conv_relu_kernel(tc, x, w0, w1, w2, b, out):
         ps = ctx.enter_context(tc.psum_pool(name="ps", bufs=1))
         ctx.enter_context(tc.manual_schedule())
 
-        x_first = sb.tile([P, PACK, TAPS * CHUNK], F32, align_bytes=512, name="x_first")
-        x_late = {c: sb.tile([P, PACK, CHUNK], F32, align_bytes=512, name="x_late%d" % c) for c in range(TAPS, X_CHUNKS)}
+        x_first = sb.tile([P, PACK, EARLY * CHUNK], F32, align_bytes=512, name="x_first")
+        x_late = {c: sb.tile([P, PACK, CHUNK], F32, align_bytes=512, name="x_late%d" % c) for c in range(EARLY, X_CHUNKS)}
         w_raw = [sb.tile([P, PACK, M], F32, align_bytes=512, name="w_raw%d" % t) for t in range(TAPS)]
         x_bf = sb.tile([P, L, PACK], BF16, align_bytes=64, name="x_bf")
         w_bf = sb.tile([P, TAPS, M, PACK], BF16, align_bytes=64, name="w_bf")
@@ -48,7 +49,8 @@ def tile_rows_conv_relu_kernel(tc, x, w0, w1, w2, b, out):
         w_scales = sb.tile([P, TAPS, M], U8, align_bytes=64, name="w_scales")
         bias_rows = sb.tile([P, G * ROWS], F32, align_bytes=64, name="bias_rows")
         bias = sb.tile([P, G * ROWS], F32, align_bytes=64, name="bias")
-        y = [sb.tile([P, G, CHUNK], F32, align_bytes=512, name="y%d" % c) for c in range(OUT_CHUNKS)]
+        y_first = sb.tile([P, G, OPEN * CHUNK], F32, align_bytes=512, name="y_first")
+        y_late = {c: sb.tile([P, G, CHUNK], F32, align_bytes=512, name="y%d" % c) for c in range(OPEN, OUT_CHUNKS)}
         acc = [[ps.tile([P, BANK], F32, name="acc%d_%d" % (g, s)) for s in range(OPEN)] for g in range(G)]
 
         def interleave(on_vector, dst, src):
@@ -100,57 +102,75 @@ def tile_rows_conv_relu_kernel(tc, x, w0, w1, w2, b, out):
                     stop=(t == TAPS - 1),
                 )
 
-        def finish(c, on_vector, stores):
-            for g in range(G):
-                bias_g = bias[:, g * ROWS : g * ROWS + 1]
-                if g in on_vector:
-                    nc.vector.tensor_scalar(
-                        out=y[c][:, g, :], in0=sums(c, g), scalar1=bias_g, scalar2=0.0, op0=ALU.add, op1=ALU.max
-                    )
-                else:
-                    nc.scalar.activation(out=y[c][:, g, :], in_=sums(c, g), func=RELU, bias=bias_g)
-                for groups in stores:
-                    if groups.stop == g + 1:
-                        nc.sync.dma_start(out=out_rows[:, groups, c * CHUNK : (c + 1) * CHUNK], in_=y[c][:, groups, :])
+        def read(on_vector, c, g):
+            dst = y_first[:, g, c * CHUNK : (c + 1) * CHUNK] if c < OPEN else y_late[c][:, g, :]
+            bias_g = bias[:, g * ROWS : g * ROWS + 1]
+            if on_vector:
+                nc.vector.tensor_scalar(out=dst, in0=sums(c, g), scalar1=bias_g, scalar2=0.0, op0=ALU.add, op1=ALU.max)
+            else:
+                nc.scalar.activation(out=dst, in_=sums(c, g), func=RELU, bias=bias_g)
 
-        nc.sync.dma_start(out=w_raw[0][:], in_=w_rows[0])
+        def finish(c):
+            for g in range(0, G, 2):
+                read(False, c, g)
+                read(True, c, g + 1)
+                nc.sync.dma_start(out=out_rows[:, g : g + 2, c * CHUNK : (c + 1) * CHUNK], in_=y_late[c][:, g : g + 2, :])
+
+        nc.sync.dma_start(out=x_first[:], in_=x_rows[:, :, : EARLY * CHUNK])
         nc.vector.memset(bias_rows[:], 0.0)
         nc.sync.dma_start(
             out=bias_rows[0:P:ROWS, :].rearrange("q (g j) -> q g j", g=G),
             in_=b.rearrange("g (q j) o -> q g (j o)", j=ROWS),
         )
-        nc.sync.dma_start(out=x_first[:], in_=x_rows[:, :, : TAPS * CHUNK])
-        for t in range(1, TAPS):
+        for t in range(TAPS):
             nc.sync.dma_start(out=w_raw[t][:], in_=w_rows[t])
-        for c in range(TAPS, X_CHUNKS):
+        for c in range(EARLY, X_CHUNKS):
             nc.sync.dma_start(out=x_late[c][:], in_=x_rows[:, :, c * CHUNK : (c + 1) * CHUNK])
 
+        for c in range(EARLY):
+            interleave(c < 2, x_bf[:, c * CHUNK : (c + 1) * CHUNK, :], x_first[:, :, c * CHUNK : (c + 1) * CHUNK])
         interleave_w(True, 0, 0, M)
-        nc.vector.transpose(out=bias[:], in_=bias_rows[:])
-        quantize_w(0, 0, M)
-        interleave(True, x_bf[:, :CHUNK, :], x_first[:, :, :CHUNK])
-        interleave(True, x_bf[:, CHUNK : 2 * CHUNK, :], x_first[:, :, CHUNK : 2 * CHUNK])
-        interleave(False, x_bf[:, 2 * CHUNK : 3 * CHUNK, :], x_first[:, :, 2 * CHUNK :])
-        for c in range(TAPS):
+        for c in range(2):
             quantize_x(c * CHUNK, (c + 1) * CHUNK)
+        interleave_w(True, 1, 0, M // 2)
+        interleave_w(False, 1, M // 2, M)
+        quantize_w(0, 0, M)
+        quantize_x(2 * CHUNK, 3 * CHUNK)
+        quantize_w(1, 0, M)
         tap(0, 0)
         tap(1, 0)
-        interleave_w(False, 1, 0, M)
         interleave_w(True, 2, 0, M // 2)
-        interleave_w(True, 2, M // 2, M)
-        quantize_w(1, 0, M)
+        interleave_w(True, 2, M // 2, 3 * M // 4)
+        interleave_w(False, 2, 3 * M // 4, M)
+        quantize_x(3 * CHUNK, 4 * CHUNK)
         quantize_w(2, 0, M // 2)
         quantize_w(2, M // 2, M)
+        nc.vector.transpose(out=bias[:], in_=bias_rows[:])
         tap(0, 1)
-        tap(0, 2)
         tap(1, 1)
+        for g in range(G):
+            tap(0, 2, [g])
+            tap(1, 2, [g])
 
-        for c in range(OUT_CHUNKS - 1):
-            prepare_late_x(c + TAPS)
-            finish(c, on_vector=(1,), stores=(slice(0, 1), slice(1, 4)))
-            tap(c + 1, TAPS - 1)
-            if c + OPEN < OUT_CHUNKS:
-                for g in range(G):
-                    for t in range(TAPS - 1):
-                        tap(c + OPEN, t, [g])
-        finish(OUT_CHUNKS - 1, on_vector=(1, 3), stores=(slice(0, 2), slice(2, 4)))
+        prepare_late_x(EARLY)
+        for g in range(G):
+            read(False, 0, g)
+            if g < 2:
+                read(True, 1, g)
+                nc.sync.dma_start(out=out_rows[:, g, : OPEN * CHUNK], in_=y_first[:, g, :])
+        for g in range(2, G):
+            read(False, 1, g)
+            nc.sync.dma_start(out=out_rows[:, g, : OPEN * CHUNK], in_=y_first[:, g, :])
+        prepare_late_x(EARLY + 1)
+        for g in range(G):
+            for t in range(TAPS):
+                tap(2, t, [g])
+            if g < 2:
+                for t in range(TAPS - 1):
+                    tap(3, t, [g])
+        for g in range(2, G):
+            for t in range(TAPS - 1):
+                tap(3, t, [g])
+        tap(3, TAPS - 1)
+        finish(2)
+        finish(3)

@@ -24,6 +24,7 @@ OUT_CHUNKS = N // CHUNK
 BANK = 512
 EARLY = 4
 OPEN = 2
+SHARE = 80
 RUN = 4
 
 
@@ -127,24 +128,19 @@ def tile_rows_conv_relu_kernel(tc, x, w0, w1, w2, b, out):
         for c in range(EARLY, X_CHUNKS):
             nc.sync.dma_start(out=x_late[c][:], in_=x_rows[:, :, c * CHUNK : (c + 1) * CHUNK])
 
-        for c in range(EARLY):
-            interleave(c < 2, x_bf[:, c * CHUNK : (c + 1) * CHUNK, :], x_first[:, :, c * CHUNK : (c + 1) * CHUNK])
+        interleave(True, x_bf[:, : 2 * CHUNK, :], x_first[:, :, : 2 * CHUNK])
+        interleave(False, x_bf[:, 2 * CHUNK : 4 * CHUNK, :], x_first[:, :, 2 * CHUNK :])
         interleave_w(True, 0, 0, M)
-        for c in range(2):
-            quantize_x(c * CHUNK, (c + 1) * CHUNK)
-        interleave_w(True, 1, 0, M // 2)
-        interleave_w(False, 1, M // 2, M)
+        quantize_x(0, 2 * CHUNK)
         quantize_w(0, 0, M)
-        quantize_x(2 * CHUNK, 3 * CHUNK)
-        quantize_w(1, 0, M)
+        quantize_x(2 * CHUNK, 4 * CHUNK)
         tap(0, 0)
         tap(1, 0)
-        interleave_w(True, 2, 0, M // 2)
-        interleave_w(True, 2, M // 2, 3 * M // 4)
-        interleave_w(False, 2, 3 * M // 4, M)
-        quantize_x(3 * CHUNK, 4 * CHUNK)
-        quantize_w(2, 0, M // 2)
-        quantize_w(2, M // 2, M)
+        interleave_w(False, 1, 0, M)
+        interleave_w(True, 2, 0, SHARE)
+        interleave_w(False, 2, SHARE, M)
+        quantize_w(1, 0, M)
+        quantize_w(2, 0, M)
         nc.vector.transpose(out=bias[:], in_=bias_rows[:])
         tap(0, 1)
         tap(1, 1)
@@ -152,7 +148,10 @@ def tile_rows_conv_relu_kernel(tc, x, w0, w1, w2, b, out):
             tap(0, 2, [g])
             tap(1, 2, [g])
 
-        prepare_late_x(EARLY)
+        lo = EARLY * CHUNK
+        interleave(True, x_bf[:, lo : lo + SHARE, :], x_late[EARLY][:, :, :SHARE])
+        interleave(False, x_bf[:, lo + SHARE : lo + CHUNK, :], x_late[EARLY][:, :, SHARE:])
+        quantize_x(lo, lo + CHUNK)
         for g in range(G):
             read(False, 0, g)
             if g < 2:

@@ -50,8 +50,7 @@ def tile_rows_conv_relu_kernel(tc, x, w0, w1, w2, b, out):
         w_scales = sb.tile([P, TAPS, M], U8, align_bytes=64, name="w_scales")
         bias_rows = sb.tile([P, G * ROWS], F32, align_bytes=64, name="bias_rows")
         bias = sb.tile([P, G * ROWS], F32, align_bytes=64, name="bias")
-        y_first = sb.tile([P, G, OPEN * CHUNK], F32, align_bytes=512, name="y_first")
-        y_late = {c: sb.tile([P, G, CHUNK], F32, align_bytes=512, name="y%d" % c) for c in range(OPEN, OUT_CHUNKS)}
+        y = [sb.tile([P, G, CHUNK], F32, align_bytes=512, name="y%d" % c) for c in range(OUT_CHUNKS)]
         acc = [[ps.tile([P, BANK], F32, name="acc%d_%d" % (g, s)) for s in range(OPEN)] for g in range(G)]
 
         def interleave(on_vector, dst, src):
@@ -104,27 +103,27 @@ def tile_rows_conv_relu_kernel(tc, x, w0, w1, w2, b, out):
                 )
 
         def read(on_vector, c, g):
-            dst = y_first[:, g, c * CHUNK : (c + 1) * CHUNK] if c < OPEN else y_late[c][:, g, :]
+            dst = y[c][:, g, :]
             bias_g = bias[:, g * ROWS : g * ROWS + 1]
             if on_vector:
                 nc.vector.tensor_scalar(out=dst, in0=sums(c, g), scalar1=bias_g, scalar2=0.0, op0=ALU.add, op1=ALU.max)
             else:
                 nc.scalar.activation(out=dst, in_=sums(c, g), func=RELU, bias=bias_g)
 
-        def finish(c):
+        def finish(c, shared):
             for g in range(0, G, 2):
                 read(False, c, g)
-                read(True, c, g + 1)
-                nc.sync.dma_start(out=out_rows[:, g : g + 2, c * CHUNK : (c + 1) * CHUNK], in_=y_late[c][:, g : g + 2, :])
+                read(shared, c, g + 1)
+                nc.sync.dma_start(out=out_rows[:, g : g + 2, c * CHUNK : (c + 1) * CHUNK], in_=y[c][:, g : g + 2, :])
 
         nc.sync.dma_start(out=x_first[:], in_=x_rows[:, :, : EARLY * CHUNK])
+        for t in range(TAPS):
+            nc.sync.dma_start(out=w_raw[t][:], in_=w_rows[t])
         nc.vector.memset(bias_rows[:], 0.0)
         nc.sync.dma_start(
             out=bias_rows[0:P:ROWS, :].rearrange("q (g j) -> q g j", g=G),
             in_=b.rearrange("g (q j) o -> q g (j o)", j=ROWS),
         )
-        for t in range(TAPS):
-            nc.sync.dma_start(out=w_raw[t][:], in_=w_rows[t])
         for c in range(EARLY, X_CHUNKS):
             nc.sync.dma_start(out=x_late[c][:], in_=x_rows[:, :, c * CHUNK : (c + 1) * CHUNK])
 
@@ -141,35 +140,22 @@ def tile_rows_conv_relu_kernel(tc, x, w0, w1, w2, b, out):
         interleave_w(False, 2, SHARE, M)
         quantize_w(1, 0, M)
         quantize_w(2, 0, M)
-        nc.vector.transpose(out=bias[:], in_=bias_rows[:])
-        tap(0, 1)
-        tap(1, 1)
-        for g in range(G):
-            tap(0, 2, [g])
-            tap(1, 2, [g])
+        for c in range(OPEN):
+            tap(c, 1)
+            tap(c, 2)
 
         lo = EARLY * CHUNK
         interleave(True, x_bf[:, lo : lo + SHARE, :], x_late[EARLY][:, :, :SHARE])
         interleave(False, x_bf[:, lo + SHARE : lo + CHUNK, :], x_late[EARLY][:, :, SHARE:])
+        nc.vector.transpose(out=bias[:], in_=bias_rows[:])
         quantize_x(lo, lo + CHUNK)
-        for g in range(G):
-            read(False, 0, g)
-            if g < 2:
-                read(True, 1, g)
-                nc.sync.dma_start(out=out_rows[:, g, : OPEN * CHUNK], in_=y_first[:, g, :])
-        for g in range(2, G):
-            read(False, 1, g)
-            nc.sync.dma_start(out=out_rows[:, g, : OPEN * CHUNK], in_=y_first[:, g, :])
+        finish(0, shared=True)
+        finish(1, shared=False)
         prepare_late_x(EARLY + 1)
-        for g in range(G):
-            for t in range(TAPS):
-                tap(2, t, [g])
-            if g < 2:
+        for c in range(OPEN, OUT_CHUNKS):
+            for g in range(G):
                 for t in range(TAPS - 1):
-                    tap(3, t, [g])
-        for g in range(2, G):
-            for t in range(TAPS - 1):
-                tap(3, t, [g])
-        tap(3, TAPS - 1)
-        finish(2)
-        finish(3)
+                    tap(c, t, [g])
+            tap(c, TAPS - 1)
+        for c in range(OPEN, OUT_CHUNKS):
+            finish(c, shared=True)

@@ -22,7 +22,7 @@ CHUNK = 128
 X_CHUNKS = L // CHUNK
 OUT_CHUNKS = N // CHUNK
 BANK = 512
-EARLY = 4
+EARLY = 3
 OPEN = 2
 SHARE = 80
 RUN = 4
@@ -116,46 +116,93 @@ def tile_rows_conv_relu_kernel(tc, x, w0, w1, w2, b, out):
                 read(shared, c, g + 1)
                 nc.sync.dma_start(out=out_rows[:, g : g + 2, c * CHUNK : (c + 1) * CHUNK], in_=y[c][:, g : g + 2, :])
 
-        nc.sync.dma_start(out=x_first[:], in_=x_rows[:, :, : EARLY * CHUNK])
-        for t in range(TAPS):
-            nc.sync.dma_start(out=w_raw[t][:], in_=w_rows[t])
-        nc.vector.memset(bias_rows[:], 0.0)
-        nc.sync.dma_start(
-            out=bias_rows[0:P:ROWS, :].rearrange("q (g j) -> q g j", g=G),
-            in_=b.rearrange("g (q j) o -> q g (j o)", j=ROWS),
-        )
-        for c in range(EARLY, X_CHUNKS):
+
+        def load_bias():
+            nc.vector.memset(bias_rows[:], 0.0)
+            nc.sync.dma_start(
+                out=bias_rows[0:P:ROWS, :].rearrange("q (g j) -> q g j", g=G),
+                in_=b.rearrange("g (q j) o -> q g (j o)", j=ROWS),
+            )
+
+        def load_x(c):
             nc.sync.dma_start(out=x_late[c][:], in_=x_rows[:, :, c * CHUNK : (c + 1) * CHUNK])
 
-        interleave(True, x_bf[:, : 2 * CHUNK, :], x_first[:, :, : 2 * CHUNK])
-        interleave(False, x_bf[:, 2 * CHUNK : 4 * CHUNK, :], x_first[:, :, 2 * CHUNK :])
-        interleave_w(True, 0, 0, M)
-        quantize_x(0, 2 * CHUNK)
-        quantize_w(0, 0, M)
-        quantize_x(2 * CHUNK, 4 * CHUNK)
-        tap(0, 0)
-        tap(1, 0)
-        interleave_w(False, 1, 0, M)
-        interleave_w(True, 2, 0, SHARE)
-        interleave_w(False, 2, SHARE, M)
-        quantize_w(1, 0, M)
-        quantize_w(2, 0, M)
-        for c in range(OPEN):
-            tap(c, 1)
-            tap(c, 2)
+        def store(c, g0, g1):
+            nc.sync.dma_start(out=out_rows[:, g0:g1, c * CHUNK : (c + 1) * CHUNK], in_=y[c][:, g0:g1, :])
 
-        lo = EARLY * CHUNK
-        interleave(True, x_bf[:, lo : lo + SHARE, :], x_late[EARLY][:, :, :SHARE])
-        interleave(False, x_bf[:, lo + SHARE : lo + CHUNK, :], x_late[EARLY][:, :, SHARE:])
-        nc.vector.transpose(out=bias[:], in_=bias_rows[:])
-        quantize_x(lo, lo + CHUNK)
-        finish(0, shared=True)
-        finish(1, shared=False)
-        prepare_late_x(EARLY + 1)
-        for c in range(OPEN, OUT_CHUNKS):
+        def copy_late(on_vector, c, lo, hi):
+            interleave(on_vector, x_bf[:, c * CHUNK + lo : c * CHUNK + hi, :], x_late[c][:, :, lo:hi])
+
+        def quantize_chunk(c):
+            quantize_x(c * CHUNK, (c + 1) * CHUNK)
+
+        def open_chunk(c):
             for g in range(G):
                 for t in range(TAPS - 1):
                     tap(c, t, [g])
-            tap(c, TAPS - 1)
-        for c in range(OPEN, OUT_CHUNKS):
-            finish(c, shared=True)
+
+        nc.sync.dma_start(out=x_first[:], in_=x_rows[:, :, : EARLY * CHUNK])
+        for t in range(TAPS):
+            nc.sync.dma_start(out=w_raw[t][:], in_=w_rows[t])
+        load_x(3)
+        load_bias()
+        load_x(4)
+        load_x(5)
+        interleave(True, x_bf[:, :CHUNK, :], x_first[:, :, :CHUNK])
+        interleave(True, x_bf[:, CHUNK : 2 * CHUNK, :], x_first[:, :, CHUNK : 2 * CHUNK])
+        interleave(False, x_bf[:, 2 * CHUNK : 3 * CHUNK, :], x_first[:, :, 2 * CHUNK :])
+        interleave_w(False, 0, 0, M)
+        quantize_chunk(0)
+        quantize_x(CHUNK, 3 * CHUNK)
+        interleave_w(True, 1, 0, M)
+        quantize_w(0, 0, M)
+        tap(0, 0)
+        tap(1, 0)
+        interleave_w(True, 2, 0, 80)
+        interleave_w(False, 2, 80, M)
+        quantize_w(1, 0, M)
+        tap(0, 1)
+        tap(1, 1)
+        quantize_w(2, 0, M)
+        tap(0, 2)
+        copy_late(True, 3, 0, 64)
+        copy_late(False, 3, 64, 128)
+        nc.vector.transpose(out=bias[:], in_=bias_rows[:])
+        quantize_chunk(3)
+        tap(1, 2)
+        copy_late(True, 4, 0, 88)
+        copy_late(False, 4, 88, 128)
+        read(False, 0, 0)
+        read(True, 0, 1)
+        read(False, 0, 2)
+        read(True, 0, 3)
+        store(0, 0, 4)
+        quantize_chunk(4)
+        tap(2, 0, [0, 1])
+        tap(2, 1, [0, 1])
+        tap(2, 0, [2, 3])
+        tap(2, 1, [2, 3])
+        tap(2, 2)
+        copy_late(True, 5, 0, 64)
+        copy_late(False, 5, 64, 128)
+        read(True, 1, 1)
+        read(False, 1, 0)
+        read(True, 1, 3)
+        read(False, 1, 2)
+        store(1, 0, 4)
+        quantize_chunk(5)
+        tap(3, 0, [0, 1])
+        tap(3, 1, [0, 1])
+        tap(3, 0, [2, 3])
+        tap(3, 1, [2, 3])
+        tap(3, 2)
+        read(False, 2, 0)
+        read(True, 2, 1)
+        read(False, 2, 2)
+        read(True, 2, 3)
+        store(2, 0, 4)
+        read(False, 3, 0)
+        read(True, 3, 1)
+        read(False, 3, 2)
+        read(True, 3, 3)
+        store(3, 0, 4)

@@ -22,7 +22,7 @@ CHUNK = 128
 X_CHUNKS = L // CHUNK
 OUT_CHUNKS = N // CHUNK
 BANK = 512
-EARLY = 3
+EARLY = 2
 OPEN = 2
 SHARE = 80
 RUN = 4
@@ -140,28 +140,31 @@ def tile_rows_conv_relu_kernel(tc, x, w0, w1, w2, b, out):
             for g in range(G):
                 for t in range(TAPS - 1):
                     tap(c, t, [g])
-
+        nc.sync.dma_start(out=w_raw[0][:], in_=w_rows[0])
         nc.sync.dma_start(out=x_first[:], in_=x_rows[:, :, : EARLY * CHUNK])
-        for t in range(TAPS):
-            nc.sync.dma_start(out=w_raw[t][:], in_=w_rows[t])
+        nc.sync.dma_start(out=w_raw[1][:], in_=w_rows[1])
+        load_x(2)
+        nc.sync.dma_start(out=w_raw[2][:], in_=w_rows[2])
         load_x(3)
         load_bias()
         load_x(4)
         load_x(5)
-        interleave(True, x_bf[:, :CHUNK, :], x_first[:, :, :CHUNK])
-        interleave(True, x_bf[:, CHUNK : 2 * CHUNK, :], x_first[:, :, CHUNK : 2 * CHUNK])
-        interleave(False, x_bf[:, 2 * CHUNK : 3 * CHUNK, :], x_first[:, :, 2 * CHUNK :])
-        interleave_w(False, 0, 0, M)
-        quantize_chunk(0)
-        quantize_x(CHUNK, 3 * CHUNK)
-        interleave_w(True, 1, 0, M)
+        interleave_w(True, 0, 0, 128)
         quantize_w(0, 0, M)
+        interleave(True, x_bf[:, 0:128, :], x_first[:, :, 0:128])
+        interleave(False, x_bf[:, 160:256, :], x_first[:, :, 160:256])
+        interleave(True, x_bf[:, 128:160, :], x_first[:, :, 128:160])
+        quantize_chunk(0)
+        quantize_chunk(1)
         tap(0, 0)
         tap(1, 0)
-        interleave_w(True, 2, 0, 80)
-        interleave_w(False, 2, 80, M)
+        interleave_w(False, 1, 0, 128)
+        copy_late(True, 2, 0, 128)
         quantize_w(1, 0, M)
         tap(0, 1)
+        interleave_w(True, 2, 0, 80)
+        interleave_w(False, 2, 80, 128)
+        quantize_chunk(2)
         tap(1, 1)
         quantize_w(2, 0, M)
         tap(0, 2)

@@ -201,11 +201,13 @@ def tile_rows_conv_relu_kernel(tc, x, w0, w1, w2, b, out):
         tap(3, 2)
         read(False, 2, 0)
         read(True, 2, 1)
+        store(2, 0, 2)
         read(False, 2, 2)
         read(True, 2, 3)
-        store(2, 0, 4)
+        store(2, 2, 4)
         read(False, 3, 0)
         read(True, 3, 1)
+        store(3, 0, 2)
         read(False, 3, 2)
         read(True, 3, 3)
-        store(3, 0, 4)
+        store(3, 2, 4)

@@ -19,13 +19,17 @@ P = 128
 PACK = 4
 ROWS = D // PACK
 CHUNK = 128
+HALF = CHUNK // 2
 X_CHUNKS = L // CHUNK
 OUT_CHUNKS = N // CHUNK
 BANK = 512
-EARLY = 2
-OPEN = 2
-SHARE = 80
+BANKS = 2
+FIRST = 2
+PAIRS = ((0, 1), (2, 3))
+ALL = range(G)
 RUN = 4
+SHARE_FIRST = 160
+SHARE_X = {3: HALF, 4: 88, 5: HALF}
 
 
 def tile_rows_conv_relu_kernel(tc, x, w0, w1, w2, b, out):
@@ -39,8 +43,8 @@ def tile_rows_conv_relu_kernel(tc, x, w0, w1, w2, b, out):
         ps = ctx.enter_context(tc.psum_pool(name="ps", bufs=1))
         ctx.enter_context(tc.manual_schedule())
 
-        x_first = sb.tile([P, PACK, EARLY * CHUNK], F32, align_bytes=512, name="x_first")
-        x_late = {c: sb.tile([P, PACK, CHUNK], F32, align_bytes=512, name="x_late%d" % c) for c in range(EARLY, X_CHUNKS)}
+        x_first = sb.tile([P, PACK, FIRST * CHUNK], F32, align_bytes=512, name="x_first")
+        x_late = {c: sb.tile([P, PACK, CHUNK], F32, align_bytes=512, name="x_late%d" % c) for c in range(FIRST, X_CHUNKS)}
         w_raw = [sb.tile([P, PACK, M], F32, align_bytes=512, name="w_raw%d" % t) for t in range(TAPS)]
         x_bf = sb.tile([P, L, PACK], BF16, align_bytes=64, name="x_bf")
         w_bf = sb.tile([P, TAPS, M, PACK], BF16, align_bytes=64, name="w_bf")
@@ -51,7 +55,13 @@ def tile_rows_conv_relu_kernel(tc, x, w0, w1, w2, b, out):
         bias_rows = sb.tile([P, G * ROWS], F32, align_bytes=64, name="bias_rows")
         bias = sb.tile([P, G * ROWS], F32, align_bytes=64, name="bias")
         y = [sb.tile([P, G, CHUNK], F32, align_bytes=512, name="y%d" % c) for c in range(OUT_CHUNKS)]
-        acc = [[ps.tile([P, BANK], F32, name="acc%d_%d" % (g, s)) for s in range(OPEN)] for g in range(G)]
+        acc = [[ps.tile([P, BANK], F32, name="acc%d_%d" % (g, s)) for s in range(BANKS)] for g in range(G)]
+
+        def load_w(t):
+            nc.sync.dma_start(out=w_raw[t][:], in_=w_rows[t])
+
+        def load_x(c):
+            nc.sync.dma_start(out=x_late[c][:], in_=x_rows[:, :, c * CHUNK : (c + 1) * CHUNK])
 
         def interleave(on_vector, dst, src):
             src = src.rearrange("p j (c i) -> p c j i", i=RUN)
@@ -61,34 +71,39 @@ def tile_rows_conv_relu_kernel(tc, x, w0, w1, w2, b, out):
             else:
                 nc.scalar.activation(out=dst, in_=src, func=COPY)
 
-        def interleave_w(on_vector, t, m0, m1):
-            interleave(on_vector, w_bf[:, t, m0:m1, :], w_raw[t][:, :, m0:m1])
+        def copy_first(on_vector, lo, hi):
+            interleave(on_vector, x_bf[:, lo:hi, :], x_first[:, :, lo:hi])
 
-        def quantize_x(lo, hi):
+        def copy_x(on_vector, c, lo, hi):
+            interleave(on_vector, x_bf[:, c * CHUNK + lo : c * CHUNK + hi, :], x_late[c][:, :, lo:hi])
+
+        def copy_x_shared(c):
+            copy_x(True, c, 0, SHARE_X[c])
+            copy_x(False, c, SHARE_X[c], CHUNK)
+
+        def copy_w(on_vector, t, lo, hi):
+            interleave(on_vector, w_bf[:, t, lo:hi, :], w_raw[t][:, :, lo:hi])
+
+        def quantize_x(c, lo=0, hi=CHUNK):
+            cols = slice(c * CHUNK + lo, c * CHUNK + hi)
             nc.vector.quantize_mx(
-                out=x_codes[:, lo:hi].bitcast(FP8X4),
-                scales=x_scales[:, lo:hi],
-                in_=x_bf[:, lo:hi, :].rearrange("p w j -> p (w j)"),
+                out=x_codes[:, cols].bitcast(FP8X4),
+                scales=x_scales[:, cols],
+                in_=x_bf[:, cols, :].rearrange("p w j -> p (w j)"),
             )
 
-        def quantize_w(t, m0, m1):
+        def quantize_w(t, lo=0, hi=M):
             nc.vector.quantize_mx(
-                out=w_codes[:, t, m0:m1].bitcast(FP8X4),
-                scales=w_scales[:, t, m0:m1],
-                in_=w_bf[:, t, m0:m1, :].rearrange("p w j -> p (w j)"),
+                out=w_codes[:, t, lo:hi].bitcast(FP8X4),
+                scales=w_scales[:, t, lo:hi],
+                in_=w_bf[:, t, lo:hi, :].rearrange("p w j -> p (w j)"),
             )
-
-        def prepare_late_x(c):
-            half = CHUNK // 2
-            for h in (0, half):
-                interleave(True, x_bf[:, c * CHUNK + h : c * CHUNK + h + half, :], x_late[c][:, :, h : h + half])
-            for h in (0, half):
-                quantize_x(c * CHUNK + h, c * CHUNK + h + half)
 
         def sums(c, g):
-            return acc[g][c % OPEN][:, (c // OPEN) * CHUNK : (c // OPEN + 1) * CHUNK]
+            lo = (c // BANKS) * CHUNK
+            return acc[g][c % BANKS][:, lo : lo + CHUNK]
 
-        def tap(c, t, groups=range(G)):
+        def tap(c, t, groups):
             cols = slice((c + t) * CHUNK, (c + t + 1) * CHUNK)
             for g in groups:
                 rows = slice(g * ROWS, (g + 1) * ROWS)
@@ -102,6 +117,12 @@ def tile_rows_conv_relu_kernel(tc, x, w0, w1, w2, b, out):
                     stop=(t == TAPS - 1),
                 )
 
+        def reopen(c):
+            for pair in PAIRS:
+                for t in range(TAPS - 1):
+                    tap(c, t, pair)
+            tap(c, TAPS - 1, ALL)
+
         def read(on_vector, c, g):
             dst = y[c][:, g, :]
             bias_g = bias[:, g * ROWS : g * ROWS + 1]
@@ -110,104 +131,70 @@ def tile_rows_conv_relu_kernel(tc, x, w0, w1, w2, b, out):
             else:
                 nc.scalar.activation(out=dst, in_=sums(c, g), func=RELU, bias=bias_g)
 
-        def finish(c, shared):
-            for g in range(0, G, 2):
-                read(False, c, g)
-                read(shared, c, g + 1)
-                nc.sync.dma_start(out=out_rows[:, g : g + 2, c * CHUNK : (c + 1) * CHUNK], in_=y[c][:, g : g + 2, :])
-
-
-        def load_bias():
-            nc.vector.memset(bias_rows[:], 0.0)
-            nc.sync.dma_start(
-                out=bias_rows[0:P:ROWS, :].rearrange("q (g j) -> q g j", g=G),
-                in_=b.rearrange("g (q j) o -> q g (j o)", j=ROWS),
-            )
-
-        def load_x(c):
-            nc.sync.dma_start(out=x_late[c][:], in_=x_rows[:, :, c * CHUNK : (c + 1) * CHUNK])
-
         def store(c, g0, g1):
             nc.sync.dma_start(out=out_rows[:, g0:g1, c * CHUNK : (c + 1) * CHUNK], in_=y[c][:, g0:g1, :])
 
-        def copy_late(on_vector, c, lo, hi):
-            interleave(on_vector, x_bf[:, c * CHUNK + lo : c * CHUNK + hi, :], x_late[c][:, :, lo:hi])
+        def read_pair(c, pair):
+            read(False, c, pair[0])
+            read(True, c, pair[1])
 
-        def quantize_chunk(c):
-            quantize_x(c * CHUNK, (c + 1) * CHUNK)
-
-        def open_chunk(c):
-            for g in range(G):
-                for t in range(TAPS - 1):
-                    tap(c, t, [g])
-        nc.sync.dma_start(out=w_raw[0][:], in_=w_rows[0])
-        nc.sync.dma_start(out=x_first[:], in_=x_rows[:, :, : EARLY * CHUNK])
-        nc.sync.dma_start(out=w_raw[1][:], in_=w_rows[1])
+        load_w(0)
+        nc.sync.dma_start(out=x_first[:], in_=x_rows[:, :, : FIRST * CHUNK])
+        load_w(1)
         load_x(2)
-        nc.sync.dma_start(out=w_raw[2][:], in_=w_rows[2])
+        load_w(2)
         load_x(3)
-        load_bias()
+        nc.vector.memset(bias_rows[:], 0.0)
+        nc.sync.dma_start(
+            out=bias_rows[0:P:ROWS, :].rearrange("q (g j) -> q g j", g=G),
+            in_=b.rearrange("g (q j) o -> q g (j o)", j=ROWS),
+        )
         load_x(4)
         load_x(5)
-        interleave_w(True, 0, 0, 128)
-        quantize_w(0, 0, M)
-        interleave(True, x_bf[:, 0:128, :], x_first[:, :, 0:128])
-        interleave(False, x_bf[:, 160:256, :], x_first[:, :, 160:256])
-        interleave(True, x_bf[:, 128:160, :], x_first[:, :, 128:160])
-        quantize_chunk(0)
-        quantize_chunk(1)
-        tap(0, 0)
-        tap(1, 0)
-        interleave_w(False, 1, 0, 128)
-        copy_late(True, 2, 0, 128)
-        quantize_w(1, 0, M)
-        tap(0, 1)
-        interleave_w(True, 2, 0, 80)
-        interleave_w(False, 2, 80, 128)
-        quantize_chunk(2)
-        tap(1, 1)
-        quantize_w(2, 0, M)
-        tap(0, 2)
-        copy_late(True, 3, 0, 64)
-        copy_late(False, 3, 64, 128)
+
+        copy_w(True, 0, 0, M)
+        quantize_w(0)
+        copy_first(True, 0, CHUNK)
+        copy_first(False, SHARE_FIRST, FIRST * CHUNK)
+        copy_first(True, CHUNK, SHARE_FIRST)
+        quantize_x(0)
+        quantize_x(1)
+        tap(0, 0, ALL)
+        tap(1, 0, ALL)
+        copy_w(False, 1, 0, M)
+        copy_x(True, 2, 0, CHUNK)
+        quantize_w(1)
+        tap(0, 1, ALL)
+        copy_w(True, 2, 0, HALF)
+        copy_w(False, 2, HALF, M)
+        quantize_x(2)
+        tap(1, 1, ALL)
+        quantize_w(2, 0, HALF)
+        quantize_w(2, HALF, M)
+        tap(0, 2, ALL)
+
+        copy_x_shared(3)
         nc.vector.transpose(out=bias[:], in_=bias_rows[:])
-        quantize_chunk(3)
-        tap(1, 2)
-        copy_late(True, 4, 0, 88)
-        copy_late(False, 4, 88, 128)
-        read(False, 0, 0)
-        read(True, 0, 1)
-        read(False, 0, 2)
-        read(True, 0, 3)
-        store(0, 0, 4)
-        quantize_chunk(4)
-        tap(2, 0, [0, 1])
-        tap(2, 1, [0, 1])
-        tap(2, 0, [2, 3])
-        tap(2, 1, [2, 3])
-        tap(2, 2)
-        copy_late(True, 5, 0, 64)
-        copy_late(False, 5, 64, 128)
-        read(True, 1, 1)
-        read(False, 1, 0)
-        read(True, 1, 3)
-        read(False, 1, 2)
-        store(1, 0, 4)
-        quantize_chunk(5)
-        tap(3, 0, [0, 1])
-        tap(3, 1, [0, 1])
-        tap(3, 0, [2, 3])
-        tap(3, 1, [2, 3])
-        tap(3, 2)
-        read(False, 2, 0)
-        read(True, 2, 1)
-        store(2, 0, 2)
-        read(False, 2, 2)
-        read(True, 2, 3)
-        store(2, 2, 4)
-        read(False, 3, 0)
-        read(True, 3, 1)
-        store(3, 0, 2)
-        read(False, 3, 2)
-        read(True, 3, 3)
-        store(3, 2, 4)
+        quantize_x(3, 0, HALF)
+        quantize_x(3, HALF, CHUNK)
+        tap(1, 2, ALL)
+
+        copy_x_shared(4)
+        for pair in PAIRS:
+            read_pair(0, pair)
+        store(0, 0, G)
+        quantize_x(4)
+        reopen(2)
+
+        copy_x_shared(5)
+        for first, second in PAIRS:
+            read(True, 1, second)
+            read(False, 1, first)
+        store(1, 0, G)
+        quantize_x(5)
+        reopen(3)
+
+        for c in range(BANKS, OUT_CHUNKS):
+            for pair in PAIRS:
+                read_pair(c, pair)
+                store(c, pair[0], pair[1] + 1)

@@ -28,8 +28,7 @@ FIRST = 2
 PAIRS = ((0, 1), (2, 3))
 ALL = range(G)
 RUN = 4
-SHARE_FIRST = 160
-SHARE_X = {3: HALF, 4: 88, 5: HALF}
+SHARE_X = {4: HALF, 5: 48}
 
 
 def tile_rows_conv_relu_kernel(tc, x, w0, w1, w2, b, out):
@@ -155,25 +154,26 @@ def tile_rows_conv_relu_kernel(tc, x, w0, w1, w2, b, out):
         copy_w(True, 0, 0, M)
         quantize_w(0)
         copy_first(True, 0, CHUNK)
-        copy_first(False, SHARE_FIRST, FIRST * CHUNK)
-        copy_first(True, CHUNK, SHARE_FIRST)
+        copy_first(False, CHUNK, FIRST * CHUNK)
         quantize_x(0)
         quantize_x(1)
         tap(0, 0, ALL)
         tap(1, 0, ALL)
         copy_w(False, 1, 0, M)
-        copy_x(True, 2, 0, CHUNK)
+        copy_x(True, 2, 0, HALF)
+        copy_x(False, 2, HALF, CHUNK)
         quantize_w(1)
         tap(0, 1, ALL)
-        copy_w(True, 2, 0, HALF)
-        copy_w(False, 2, HALF, M)
+        copy_w(False, 2, 0, HALF)
+        copy_w(True, 2, HALF, M)
         quantize_x(2)
         tap(1, 1, ALL)
         quantize_w(2, 0, HALF)
         quantize_w(2, HALF, M)
         tap(0, 2, ALL)
 
-        copy_x_shared(3)
+        copy_x(False, 3, 0, HALF)
+        copy_x(True, 3, HALF, CHUNK)
         nc.vector.transpose(out=bias[:], in_=bias_rows[:])
         quantize_x(3, 0, HALF)
         quantize_x(3, HALF, CHUNK)

@@ -22,13 +22,14 @@ CHUNK = 128
 HALF = CHUNK // 2
 X_CHUNKS = L // CHUNK
 OUT_CHUNKS = N // CHUNK
+BIAS_STEP = ROWS // G
 BANK = 512
 BANKS = 2
-FIRST = 2
+FIRST = 3
 PAIRS = ((0, 1), (2, 3))
 ALL = range(G)
 RUN = 4
-SHARE_X = {4: HALF, 5: 48}
+SHARE_X = {4: HALF, 5: HALF}
 
 
 def tile_rows_conv_relu_kernel(tc, x, w0, w1, w2, b, out):
@@ -51,8 +52,8 @@ def tile_rows_conv_relu_kernel(tc, x, w0, w1, w2, b, out):
         x_scales = sb.tile([P, L], U8, align_bytes=64, name="x_scales")
         w_codes = sb.tile([P, TAPS, M], U32, align_bytes=64, name="w_codes")
         w_scales = sb.tile([P, TAPS, M], U8, align_bytes=64, name="w_scales")
-        bias_rows = sb.tile([P, G * ROWS], F32, align_bytes=64, name="bias_rows")
-        bias = sb.tile([P, G * ROWS], F32, align_bytes=64, name="bias")
+        bias_rows = sb.tile([P, ROWS], F32, align_bytes=64, name="bias_rows")
+        bias = sb.tile([P, ROWS], F32, align_bytes=64, name="bias")
         y = [sb.tile([P, G, CHUNK], F32, align_bytes=512, name="y%d" % c) for c in range(OUT_CHUNKS)]
         acc = [[ps.tile([P, BANK], F32, name="acc%d_%d" % (g, s)) for s in range(BANKS)] for g in range(G)]
 
@@ -124,7 +125,7 @@ def tile_rows_conv_relu_kernel(tc, x, w0, w1, w2, b, out):
 
         def read(on_vector, c, g):
             dst = y[c][:, g, :]
-            bias_g = bias[:, g * ROWS : g * ROWS + 1]
+            bias_g = bias[:, g * BIAS_STEP : g * BIAS_STEP + 1]
             if on_vector:
                 nc.vector.tensor_scalar(out=dst, in0=sums(c, g), scalar1=bias_g, scalar2=0.0, op0=ALU.add, op1=ALU.max)
             else:
@@ -137,37 +138,36 @@ def tile_rows_conv_relu_kernel(tc, x, w0, w1, w2, b, out):
             read(False, c, pair[0])
             read(True, c, pair[1])
 
-        load_w(0)
         nc.sync.dma_start(out=x_first[:], in_=x_rows[:, :, : FIRST * CHUNK])
-        load_w(1)
-        load_x(2)
-        load_w(2)
+        for t in range(TAPS):
+            load_w(t)
         load_x(3)
         nc.vector.memset(bias_rows[:], 0.0)
         nc.sync.dma_start(
-            out=bias_rows[0:P:ROWS, :].rearrange("q (g j) -> q g j", g=G),
+            out=bias_rows[0:P:BIAS_STEP, :],
             in_=b.rearrange("g (q j) o -> q g (j o)", j=ROWS),
         )
         load_x(4)
         load_x(5)
 
-        copy_w(True, 0, 0, M)
-        quantize_w(0)
         copy_first(True, 0, CHUNK)
-        copy_first(False, CHUNK, FIRST * CHUNK)
+        copy_first(False, 2 * CHUNK, FIRST * CHUNK)
+        copy_first(True, CHUNK, 2 * CHUNK)
         quantize_x(0)
+        copy_w(False, 0, 0, M)
+        quantize_x(2)
         quantize_x(1)
+        copy_w(True, 1, HALF, M)
+        copy_w(False, 1, 0, HALF)
+        quantize_w(0)
         tap(0, 0, ALL)
         tap(1, 0, ALL)
-        copy_w(False, 1, 0, M)
-        copy_x(True, 2, 0, HALF)
-        copy_x(False, 2, HALF, CHUNK)
-        quantize_w(1)
+        quantize_w(1, 0, HALF)
+        quantize_w(1, HALF, M)
         tap(0, 1, ALL)
+        tap(1, 1, ALL)
         copy_w(False, 2, 0, HALF)
         copy_w(True, 2, HALF, M)
-        quantize_x(2)
-        tap(1, 1, ALL)
         quantize_w(2, 0, HALF)
         quantize_w(2, HALF, M)
         tap(0, 2, ALL)
@@ -182,7 +182,7 @@ def tile_rows_conv_relu_kernel(tc, x, w0, w1, w2, b, out):
         copy_x_shared(4)
         for pair in PAIRS:
             read_pair(0, pair)
-        store(0, 0, G)
+            store(0, pair[0], pair[1] + 1)
         quantize_x(4)
         reopen(2)
 

@@ -135,8 +135,8 @@ def tile_rows_conv_relu_kernel(tc, x, w0, w1, w2, b, out):
             nc.sync.dma_start(out=out_rows[:, g0:g1, c * CHUNK : (c + 1) * CHUNK], in_=y[c][:, g0:g1, :])
 
         def read_pair(c, pair):
-            read(False, c, pair[0])
-            read(True, c, pair[1])
+            read(True, c, pair[0])
+            read(False, c, pair[1])
 
         nc.sync.dma_start(out=x_first[:], in_=x_rows[:, :, : FIRST * CHUNK])
         for t in range(TAPS):
@@ -183,15 +183,16 @@ def tile_rows_conv_relu_kernel(tc, x, w0, w1, w2, b, out):
         for pair in PAIRS:
             read_pair(0, pair)
             store(0, pair[0], pair[1] + 1)
-        quantize_x(4)
+        quantize_x(4, 0, HALF)
+        quantize_x(4, HALF, CHUNK)
         reopen(2)
 
         copy_x_shared(5)
-        for first, second in PAIRS:
-            read(True, 1, second)
-            read(False, 1, first)
+        for pair in PAIRS:
+            read_pair(1, pair)
         store(1, 0, G)
-        quantize_x(5)
+        quantize_x(5, 0, HALF)
+        quantize_x(5, HALF, CHUNK)
         reopen(3)
 
         for c in range(BANKS, OUT_CHUNKS):

@@ -172,8 +172,8 @@ def tile_rows_conv_relu_kernel(tc, x, w0, w1, w2, b, out):
         quantize_w(2, HALF, M)
         tap(0, 2, ALL)
 
-        copy_x(False, 3, 0, HALF)
-        copy_x(True, 3, HALF, CHUNK)
+        copy_x(True, 3, 0, HALF)
+        copy_x(False, 3, HALF, CHUNK)
         nc.vector.transpose(out=bias[:], in_=bias_rows[:])
         quantize_x(3, 0, HALF)
         quantize_x(3, HALF, CHUNK)

@@ -29,7 +29,7 @@ FIRST = 3
 PAIRS = ((0, 1), (2, 3))
 ALL = range(G)
 RUN = 4
-SHARE_X = {4: HALF, 5: HALF}
+SHARE_X = {4: HALF, 5: 84}
 
 
 def tile_rows_conv_relu_kernel(tc, x, w0, w1, w2, b, out):

@@ -29,7 +29,7 @@ FIRST = 3
 PAIRS = ((0, 1), (2, 3))
 ALL = range(G)
 RUN = 4
-SHARE_X = {4: HALF, 5: 84}
+SHARE = 80
 
 
 def tile_rows_conv_relu_kernel(tc, x, w0, w1, w2, b, out):
@@ -78,8 +78,8 @@ def tile_rows_conv_relu_kernel(tc, x, w0, w1, w2, b, out):
             interleave(on_vector, x_bf[:, c * CHUNK + lo : c * CHUNK + hi, :], x_late[c][:, :, lo:hi])
 
         def copy_x_shared(c):
-            copy_x(True, c, 0, SHARE_X[c])
-            copy_x(False, c, SHARE_X[c], CHUNK)
+            copy_x(True, c, 0, SHARE)
+            copy_x(False, c, SHARE, CHUNK)
 
         def copy_w(on_vector, t, lo, hi):
             interleave(on_vector, w_bf[:, t, lo:hi, :], w_raw[t][:, :, lo:hi])
@@ -118,10 +118,13 @@ def tile_rows_conv_relu_kernel(tc, x, w0, w1, w2, b, out):
                 )
 
         def reopen(c):
-            for pair in PAIRS:
-                for t in range(TAPS - 1):
-                    tap(c, t, pair)
-            tap(c, TAPS - 1, ALL)
+            first, second = PAIRS
+            tap(c, 0, first)
+            tap(c, 1, first)
+            tap(c, 0, second)
+            tap(c, 2, first)
+            tap(c, 1, second)
+            tap(c, 2, second)
 
         def read(on_vector, c, g):
             dst = y[c][:, g, :]
@@ -138,23 +141,32 @@ def tile_rows_conv_relu_kernel(tc, x, w0, w1, w2, b, out):
             read(True, c, pair[0])
             read(False, c, pair[1])
 
+        def quantize_x_halves(c):
+            quantize_x(c, 0, HALF)
+            quantize_x(c, HALF, CHUNK)
+
+        def empty(c):
+            for pair in PAIRS:
+                read_pair(c, pair)
+                store(c, pair[0], pair[1] + 1)
+
         nc.sync.dma_start(out=x_first[:], in_=x_rows[:, :, : FIRST * CHUNK])
         for t in range(TAPS):
             load_w(t)
-        load_x(3)
         nc.vector.memset(bias_rows[:], 0.0)
         nc.sync.dma_start(
             out=bias_rows[0:P:BIAS_STEP, :],
             in_=b.rearrange("g (q j) o -> q g (j o)", j=ROWS),
         )
-        load_x(4)
-        load_x(5)
+        for c in range(FIRST, X_CHUNKS):
+            load_x(c)
 
         copy_first(True, 0, CHUNK)
         copy_first(False, 2 * CHUNK, FIRST * CHUNK)
         copy_first(True, CHUNK, 2 * CHUNK)
         quantize_x(0)
-        copy_w(False, 0, 0, M)
+        copy_w(True, 0, HALF, M)
+        copy_w(False, 0, 0, HALF)
         quantize_x(2)
         quantize_x(1)
         copy_w(True, 1, HALF, M)
@@ -162,40 +174,26 @@ def tile_rows_conv_relu_kernel(tc, x, w0, w1, w2, b, out):
         quantize_w(0)
         tap(0, 0, ALL)
         tap(1, 0, ALL)
-        quantize_w(1, 0, HALF)
         quantize_w(1, HALF, M)
+
+        copy_w(True, 2, 0, SHARE)
+        copy_w(False, 2, SHARE, M)
+        quantize_w(1, 0, HALF)
         tap(0, 1, ALL)
         tap(1, 1, ALL)
-        copy_w(False, 2, 0, HALF)
-        copy_w(True, 2, HALF, M)
+        nc.vector.transpose(out=bias[:], in_=bias_rows[:])
         quantize_w(2, 0, HALF)
         quantize_w(2, HALF, M)
         tap(0, 2, ALL)
 
-        copy_x(True, 3, 0, HALF)
-        copy_x(False, 3, HALF, CHUNK)
-        nc.vector.transpose(out=bias[:], in_=bias_rows[:])
-        quantize_x(3, 0, HALF)
-        quantize_x(3, HALF, CHUNK)
+        copy_x_shared(3)
+        quantize_x_halves(3)
         tap(1, 2, ALL)
 
-        copy_x_shared(4)
-        for pair in PAIRS:
-            read_pair(0, pair)
-            store(0, pair[0], pair[1] + 1)
-        quantize_x(4, 0, HALF)
-        quantize_x(4, HALF, CHUNK)
-        reopen(2)
-
-        copy_x_shared(5)
-        for pair in PAIRS:
-            read_pair(1, pair)
-        store(1, 0, G)
-        quantize_x(5, 0, HALF)
-        quantize_x(5, HALF, CHUNK)
-        reopen(3)
-
         for c in range(BANKS, OUT_CHUNKS):
-            for pair in PAIRS:
-                read_pair(c, pair)
-                store(c, pair[0], pair[1] + 1)
+            copy_x_shared(c + TAPS - 1)
+            empty(c - BANKS)
+            quantize_x_halves(c + TAPS - 1)
+            reopen(c)
+        for c in range(BANKS, OUT_CHUNKS):
+            empty(c)

@@ -29,7 +29,6 @@ FIRST = 3
 PAIRS = ((0, 1), (2, 3))
 ALL = range(G)
 RUN = 4
-SHARE = 80
 
 
 def tile_rows_conv_relu_kernel(tc, x, w0, w1, w2, b, out):
@@ -78,8 +77,8 @@ def tile_rows_conv_relu_kernel(tc, x, w0, w1, w2, b, out):
             interleave(on_vector, x_bf[:, c * CHUNK + lo : c * CHUNK + hi, :], x_late[c][:, :, lo:hi])
 
         def copy_x_shared(c):
-            copy_x(True, c, 0, SHARE)
-            copy_x(False, c, SHARE, CHUNK)
+            copy_x(True, c, 0, HALF)
+            copy_x(False, c, HALF, CHUNK)
 
         def copy_w(on_vector, t, lo, hi):
             interleave(on_vector, w_bf[:, t, lo:hi, :], w_raw[t][:, :, lo:hi])
@@ -174,17 +173,16 @@ def tile_rows_conv_relu_kernel(tc, x, w0, w1, w2, b, out):
         quantize_w(0)
         tap(0, 0, ALL)
         tap(1, 0, ALL)
-        quantize_w(1, HALF, M)
 
-        copy_w(True, 2, 0, SHARE)
-        copy_w(False, 2, SHARE, M)
-        quantize_w(1, 0, HALF)
+        copy_w(True, 2, 0, HALF)
+        copy_w(False, 2, HALF, M)
+        quantize_w(1)
         tap(0, 1, ALL)
-        tap(1, 1, ALL)
         nc.vector.transpose(out=bias[:], in_=bias_rows[:])
         quantize_w(2, 0, HALF)
         quantize_w(2, HALF, M)
         tap(0, 2, ALL)
+        tap(1, 1, ALL)
 
         copy_x_shared(3)
         quantize_x_halves(3)

@@ -28,6 +28,7 @@ BANKS = 2
 FIRST = 3
 PAIRS = ((0, 1), (2, 3))
 ALL = range(G)
+SHARE = 72
 RUN = 4
 
 
@@ -76,9 +77,9 @@ def tile_rows_conv_relu_kernel(tc, x, w0, w1, w2, b, out):
         def copy_x(on_vector, c, lo, hi):
             interleave(on_vector, x_bf[:, c * CHUNK + lo : c * CHUNK + hi, :], x_late[c][:, :, lo:hi])
 
-        def copy_x_shared(c):
-            copy_x(True, c, 0, HALF)
-            copy_x(False, c, HALF, CHUNK)
+        def copy_x_shared(c, share):
+            copy_x(True, c, 0, share)
+            copy_x(False, c, share, CHUNK)
 
         def copy_w(on_vector, t, lo, hi):
             interleave(on_vector, w_bf[:, t, lo:hi, :], w_raw[t][:, :, lo:hi])
@@ -174,8 +175,8 @@ def tile_rows_conv_relu_kernel(tc, x, w0, w1, w2, b, out):
         tap(0, 0, ALL)
         tap(1, 0, ALL)
 
-        copy_w(True, 2, 0, HALF)
-        copy_w(False, 2, HALF, M)
+        copy_w(True, 2, 0, SHARE)
+        copy_w(False, 2, SHARE, M)
         quantize_w(1)
         tap(0, 1, ALL)
         nc.vector.transpose(out=bias[:], in_=bias_rows[:])
@@ -184,12 +185,12 @@ def tile_rows_conv_relu_kernel(tc, x, w0, w1, w2, b, out):
         tap(0, 2, ALL)
         tap(1, 1, ALL)
 
-        copy_x_shared(3)
+        copy_x_shared(3, SHARE)
         quantize_x_halves(3)
         tap(1, 2, ALL)
 
         for c in range(BANKS, OUT_CHUNKS):
-            copy_x_shared(c + TAPS - 1)
+            copy_x_shared(c + TAPS - 1, HALF)
             empty(c - BANKS)
             quantize_x_halves(c + TAPS - 1)
             reopen(c)

@@ -28,6 +28,7 @@ BANKS = 2
 FIRST = 3
 PAIRS = ((0, 1), (2, 3))
 ALL = range(G)
+W2_SHARE = 80
 SHARE = 72
 RUN = 4
 
@@ -77,9 +78,9 @@ def tile_rows_conv_relu_kernel(tc, x, w0, w1, w2, b, out):
         def copy_x(on_vector, c, lo, hi):
             interleave(on_vector, x_bf[:, c * CHUNK + lo : c * CHUNK + hi, :], x_late[c][:, :, lo:hi])
 
-        def copy_x_shared(c, share):
-            copy_x(True, c, 0, share)
-            copy_x(False, c, share, CHUNK)
+        def copy_x_shared(c):
+            copy_x(True, c, 0, SHARE)
+            copy_x(False, c, SHARE, CHUNK)
 
         def copy_w(on_vector, t, lo, hi):
             interleave(on_vector, w_bf[:, t, lo:hi, :], w_raw[t][:, :, lo:hi])
@@ -153,12 +154,13 @@ def tile_rows_conv_relu_kernel(tc, x, w0, w1, w2, b, out):
         nc.sync.dma_start(out=x_first[:], in_=x_rows[:, :, : FIRST * CHUNK])
         for t in range(TAPS):
             load_w(t)
+        load_x(FIRST)
         nc.vector.memset(bias_rows[:], 0.0)
         nc.sync.dma_start(
             out=bias_rows[0:P:BIAS_STEP, :],
             in_=b.rearrange("g (q j) o -> q g (j o)", j=ROWS),
         )
-        for c in range(FIRST, X_CHUNKS):
+        for c in range(FIRST + 1, X_CHUNKS):
             load_x(c)
 
         copy_first(True, 0, CHUNK)
@@ -175,22 +177,22 @@ def tile_rows_conv_relu_kernel(tc, x, w0, w1, w2, b, out):
         tap(0, 0, ALL)
         tap(1, 0, ALL)
 
-        copy_w(True, 2, 0, SHARE)
-        copy_w(False, 2, SHARE, M)
+        copy_w(True, 2, 0, W2_SHARE)
+        copy_w(False, 2, W2_SHARE, M)
         quantize_w(1)
         tap(0, 1, ALL)
-        nc.vector.transpose(out=bias[:], in_=bias_rows[:])
         quantize_w(2, 0, HALF)
         quantize_w(2, HALF, M)
         tap(0, 2, ALL)
         tap(1, 1, ALL)
 
-        copy_x_shared(3, SHARE)
+        copy_x_shared(3)
+        nc.vector.transpose(out=bias[:], in_=bias_rows[:])
         quantize_x_halves(3)
         tap(1, 2, ALL)
 
         for c in range(BANKS, OUT_CHUNKS):
-            copy_x_shared(c + TAPS - 1, HALF)
+            copy_x_shared(c + TAPS - 1)
             empty(c - BANKS)
             quantize_x_halves(c + TAPS - 1)
             reopen(c)

from contextlib import ExitStack

import concourse.mybir as mybir

G, D, M, N, L = 4, 128, 128, 512, 768
TAPS = 3
FLOPS = 2 * G * TAPS * D * M * N

F32 = mybir.dt.float32
BF16 = mybir.dt.bfloat16
U32 = mybir.dt.uint32
U8 = mybir.dt.uint8
FP8X4 = mybir.dt.float8_e4m3fn_x4
COPY = mybir.ActivationFunctionType.Copy
RELU = mybir.ActivationFunctionType.Relu
ALU = mybir.AluOpType

P = 128
PACK = 4
ROWS = D // PACK
CHUNK = 128
HALF = CHUNK // 2
X_CHUNKS = L // CHUNK
OUT_CHUNKS = N // CHUNK
BIAS_STEP = ROWS // G
BANK = 512
BANKS = 2
FIRST = 3
PAIRS = ((0, 1), (2, 3))
ALL = range(G)
W2_SHARE = 80
SHARE = 72
RUN = 4


def tile_rows_conv_relu_kernel(tc, x, w0, w1, w2, b, out):
    nc = tc.nc
    x_rows = x.rearrange("g (p j) l -> (g p) j l", j=PACK)
    out_rows = out.rearrange("g m n -> m g n")
    w_rows = [w.rearrange("g (p j) m -> (g p) j m", j=PACK) for w in (w0, w1, w2)]

    with ExitStack() as ctx:
        sb = ctx.enter_context(tc.tile_pool(name="sb", bufs=1))
        ps = ctx.enter_context(tc.psum_pool(name="ps", bufs=1))
        ctx.enter_context(tc.manual_schedule())

        x_first = sb.tile([P, PACK, FIRST * CHUNK], F32, align_bytes=512, name="x_first")
        x_late = {c: sb.tile([P, PACK, CHUNK], F32, align_bytes=512, name="x_late%d" % c) for c in range(FIRST, X_CHUNKS)}
        w_raw = [sb.tile([P, PACK, M], F32, align_bytes=512, name="w_raw%d" % t) for t in range(TAPS)]
        x_bf = sb.tile([P, L, PACK], BF16, align_bytes=64, name="x_bf")
        w_bf = sb.tile([P, TAPS, M, PACK], BF16, align_bytes=64, name="w_bf")
        x_codes = sb.tile([P, L], U32, align_bytes=64, name="x_codes")
        x_scales = sb.tile([P, L], U8, align_bytes=64, name="x_scales")
        w_codes = sb.tile([P, TAPS, M], U32, align_bytes=64, name="w_codes")
        w_scales = sb.tile([P, TAPS, M], U8, align_bytes=64, name="w_scales")
        bias_rows = sb.tile([P, ROWS], F32, align_bytes=64, name="bias_rows")
        bias = sb.tile([P, ROWS], F32, align_bytes=64, name="bias")
        y = [sb.tile([P, G, CHUNK], F32, align_bytes=512, name="y%d" % c) for c in range(OUT_CHUNKS)]
        acc = [[ps.tile([P, BANK], F32, name="acc%d_%d" % (g, s)) for s in range(BANKS)] for g in range(G)]

        def load_w(t):
            nc.sync.dma_start(out=w_raw[t][:], in_=w_rows[t])

        def load_x(c):
            nc.sync.dma_start(out=x_late[c][:], in_=x_rows[:, :, c * CHUNK : (c + 1) * CHUNK])

        def interleave(on_vector, dst, src):
            src = src.rearrange("p j (c i) -> p c j i", i=RUN)
            dst = dst.rearrange("p (c i) j -> p c j i", i=RUN)
            if on_vector:
                nc.vector.tensor_copy(out=dst, in_=src)
            else:
                nc.scalar.activation(out=dst, in_=src, func=COPY)

        def copy_first(on_vector, lo, hi):
            interleave(on_vector, x_bf[:, lo:hi, :], x_first[:, :, lo:hi])

        def copy_x(on_vector, c, lo, hi):
            interleave(on_vector, x_bf[:, c * CHUNK + lo : c * CHUNK + hi, :], x_late[c][:, :, lo:hi])

        def copy_x_shared(c):
            copy_x(True, c, 0, SHARE)
            copy_x(False, c, SHARE, CHUNK)

        def copy_w(on_vector, t, lo, hi):
            interleave(on_vector, w_bf[:, t, lo:hi, :], w_raw[t][:, :, lo:hi])

        def quantize_x(c, lo=0, hi=CHUNK):
            cols = slice(c * CHUNK + lo, c * CHUNK + hi)
            nc.vector.quantize_mx(
                out=x_codes[:, cols].bitcast(FP8X4),
                scales=x_scales[:, cols],
                in_=x_bf[:, cols, :].rearrange("p w j -> p (w j)"),
            )

        def quantize_w(t, lo=0, hi=M):
            nc.vector.quantize_mx(
                out=w_codes[:, t, lo:hi].bitcast(FP8X4),
                scales=w_scales[:, t, lo:hi],
                in_=w_bf[:, t, lo:hi, :].rearrange("p w j -> p (w j)"),
            )

        def sums(c, g):
            lo = (c // BANKS) * CHUNK
            return acc[g][c % BANKS][:, lo : lo + CHUNK]

        def tap(c, t, groups):
            cols = slice((c + t) * CHUNK, (c + t + 1) * CHUNK)
            for g in groups:
                rows = slice(g * ROWS, (g + 1) * ROWS)
                nc.tensor.matmul_mx(
                    out=sums(c, g),
                    lhsT=w_codes[rows, t, :].bitcast(FP8X4),
                    lhsT_scale=w_scales[rows, t, :],
                    rhs=x_codes[rows, cols].bitcast(FP8X4),
                    rhs_scale=x_scales[rows, cols],
                    start=(t == 0),
                    stop=(t == TAPS - 1),
                )

        def reopen(c):
            first, second = PAIRS
            tap(c, 0, first)
            tap(c, 1, first)
            tap(c, 0, second)
            tap(c, 2, first)
            tap(c, 1, second)
            tap(c, 2, second)

        def read(on_vector, c, g):
            dst = y[c][:, g, :]
            bias_g = bias[:, g * BIAS_STEP : g * BIAS_STEP + 1]
            if on_vector:
                nc.vector.tensor_scalar(out=dst, in0=sums(c, g), scalar1=bias_g, scalar2=0.0, op0=ALU.add, op1=ALU.max)
            else:
                nc.scalar.activation(out=dst, in_=sums(c, g), func=RELU, bias=bias_g)

        def store(c, g0, g1):
            nc.sync.dma_start(out=out_rows[:, g0:g1, c * CHUNK : (c + 1) * CHUNK], in_=y[c][:, g0:g1, :])

        def read_pair(c, pair):
            read(True, c, pair[0])
            read(False, c, pair[1])

        def quantize_x_halves(c):
            quantize_x(c, 0, HALF)
            quantize_x(c, HALF, CHUNK)

        def empty(c):
            for pair in PAIRS:
                read_pair(c, pair)
                store(c, pair[0], pair[1] + 1)

        nc.sync.dma_start(out=x_first[:], in_=x_rows[:, :, : FIRST * CHUNK])
        for t in range(TAPS):
            load_w(t)
        load_x(FIRST)
        nc.vector.memset(bias_rows[:], 0.0)
        nc.sync.dma_start(
            out=bias_rows[0:P:BIAS_STEP, :],
            in_=b.rearrange("g (q j) o -> q g (j o)", j=ROWS),
        )
        for c in range(FIRST + 1, X_CHUNKS):
            load_x(c)

        copy_first(True, 0, CHUNK)
        copy_first(False, 2 * CHUNK, FIRST * CHUNK)
        copy_first(True, CHUNK, 2 * CHUNK)
        quantize_x(0)
        copy_w(True, 0, HALF, M)
        copy_w(False, 0, 0, HALF)
        quantize_x(2)
        quantize_x(1)
        copy_w(True, 1, HALF, M)
        copy_w(False, 1, 0, HALF)
        quantize_w(0)
        tap(0, 0, ALL)
        tap(1, 0, ALL)

        copy_w(True, 2, 0, W2_SHARE)
        copy_w(False, 2, W2_SHARE, M)
        quantize_w(1)
        tap(0, 1, ALL)
        quantize_w(2, 0, HALF)
        quantize_w(2, HALF, M)
        tap(0, 2, ALL)
        tap(1, 1, ALL)

        copy_x_shared(3)
        nc.vector.transpose(out=bias[:], in_=bias_rows[:])
        quantize_x_halves(3)
        tap(1, 2, ALL)

        for c in range(BANKS, OUT_CHUNKS):
            copy_x_shared(c + TAPS - 1)
            empty(c - BANKS)
            quantize_x_halves(c + TAPS - 1)
            reopen(c)
        for c in range(BANKS, OUT_CHUNKS):
            empty(c)
